import numpy as np, ml_dtypes
CORES = [9,25,41,57]
N = 4
BF = ml_dtypes.bfloat16
def gentries(a):
    return np.ascontiguousarray(a.reshape(8, 16, -1).transpose(0, 2, 1)).reshape(8, -1)
def gtable(e):
    e = np.asarray(e); return np.ascontiguousarray(e.reshape(8, -1, 16).transpose(0, 2, 1)).reshape(128, -1).astype(np.int32)
V, W, SH, CH, RO = 256, 4096, 2, 2, 4
def parts(rng):
    s = rng.integers(0, 256, (N, 8, 16, W), dtype=np.uint8); x = rng.integers(0, 256, (N, 8, 16, V), dtype=np.uint8)
    r = rng.integers(0, 256, (N, 8, 16, V)); r = np.where(rng.random((N, 8, 1, V)) < 0.5, r, 64 + (r >> 1))
    nx = rng.integers(0, V, (N, 8, V)); sr = rng.integers(0, V, (N, 8, V)); ft = rng.integers(17000, 27000, (N, 8, V))
    return s, r, x, nx, sr, ft
def pack(s, r, x, nx, sr, ft):
    return {"prof": s.reshape(N, 128, W).astype(np.float32).astype(BF), "resid": np.ascontiguousarray(r.reshape(N, 128, V)).astype(np.int32), "obs": x.reshape(N, 128, V).astype(np.float32).astype(BF),
            "nx0": np.stack([gtable(a) for a in nx]), "src0": np.stack([gtable(a) for a in sr]), "fit0": np.ascontiguousarray(ft.reshape(N, 8, V)).astype(np.int32)}
def setup_inputs(rng):
    return pack(*parts(rng))
def setup_inputs_spread(rng):
    s = np.minimum(np.exp2(8 * rng.random((N, 8, 1, W))) * rng.random((N, 8, 16, W), dtype=np.float32), 255).astype(np.uint8)
    x = np.minimum(np.exp2(8 * rng.random((N, 8, 1, V))) * rng.random((N, 8, 16, V)), 255).astype(np.uint8)
    r = np.minimum(np.exp2(8 * rng.random((1, 8, 16, 1))) * rng.random((N, 8, 16, V)), 255).astype(np.int64)
    nx = np.minimum((V * rng.random((N, 8, V)) ** 3).astype(np.int64), V - 1); sr = V - 1 - np.minimum((V * rng.random((N, 8, V)) ** 3).astype(np.int64), V - 1)
    ft = np.minimum(np.exp2(16 * rng.random((N, 8, V)) ** 0.5), 65535).astype(np.int64)
    return pack(s, r, x, nx, sr, ft)
def setup_inputs_ends(rng):
    s, r, x, nx, sr, ft = parts(rng)
    s = 255 * rng.integers(0, 2, (N, 8, 16, W), dtype=np.uint8); x = 255 * rng.integers(0, 2, (N, 8, 16, V), dtype=np.uint8)
    cnt = np.clip(np.array([8, 16, 8, 0, 8, 16, 8, 8])[None, :, None] + rng.integers(-1, 2, (N, 8, V)), 0, 16)
    r = np.where(np.argsort(rng.random((N, 8, 16, V)), axis=2) < cnt[:, :, None, :], 255, 0)
    alt = 255 * (np.arange(16) & 1); r[:, 7, :, 0] = alt; r[:, 7, :, V - 1] = 255 - alt; r[N - 1, 7, 15, V - 1] = 255
    for q in range(N):
        for g in range(8):
            if (N - 1 - q + 7 - g) % 2 == 0:
                bit = rng.permutation(np.array([0, 1] + [int(b) for b in rng.integers(0, 2, 14)])).astype(np.uint8); row = (255 * bit)[:, None]
                s[q, g] = row; kind = rng.integers(0, 4, V); kind[0] = 0; kind[V - 1] = 0
                x[q, g] = np.where(kind[None, :] < 2, 255 - row, np.where(kind[None, :] == 2, row, x[q, g]))
    ft = np.where(rng.random((N, 8, V)) < 0.7, 65535, 0); ft[:, :, 0] = 65535; ft[:, :, V - 1] = 65535
    nx = np.where(rng.random((N, 8, V)) < 0.8, (V - 1) * rng.integers(0, 2, (N, 8, V)), nx); sr = np.where(rng.random((N, 8, V)) < 0.8, (V - 1) * rng.integers(0, 2, (N, 8, V)), sr)
    nx[:, :, V - 1] = V - 1; sr[:, :, V - 1] = 0
    return pack(s, r, x, nx, sr, ft)
def setup_inputs_corners(rng):
    s, r, x, nx, sr, ft = parts(rng); own = np.arange(V)
    for q in range(N):
        r[q, 0:2] = rng.integers(0, 8, (2, 16, V)) if q % 2 == 0 else rng.integers(248, 256, (2, 16, V))
    v = rng.integers(0, 2, (N, 2, 8, V)); e = 128 + np.concatenate([v, -v], axis=2)
    e = np.take_along_axis(e, np.argsort(rng.random(e.shape), axis=2), 2)
    d = np.where((own & 1) == 1, rng.choice(np.array([-129, -128, -127, -1, 0, 1, 126, 127, 128]), (N, 2, V)), 0)
    e[:, :, 0] += d >> 1; e[:, :, 15] += d - (d >> 1); r[:, 2:4] = e
    nx[:, 2:4] = 2 * rng.integers(0, V // 2, (N, 2, V)); sr[:, 2:4] = 2 * rng.integers(0, V // 2, (N, 2, V))
    top = rng.random((N, 1, V)) < 0.5; low = np.zeros((N, 16, V), np.int64)
    np.put_along_axis(low, rng.integers(0, 16, (N, 1, V)), rng.choice(np.array([0, 0, 1, 2, 100, 254, 255]), (N, 1, V)), 1)
    r[:, 4] = np.where(top, 255 - low, low)
    for q in range(N):
        for g in range(8):
            m = (q + g) % 6
            if g not in (2, 3):
                if m == 0: nx[q, g] = own; sr[q, g] = own
                if m == 1: nx[q, g] = 0; sr[q, g] = V - 1
                if m == 2: nx[q, g] = V - 1; sr[q, g] = 0
                if m == 3: nx[q, g] = own; sr[q, g] = (own + 1) % V
                if m == 4: nx[q, g] = np.stack([0 * own, 0 * own + V - 1, own])[rng.integers(0, 3, V), own]
            m = (2 * q + g) % 5
            if m == 0: ft[q, g] = 0
            if m == 1: ft[q, g] = 65535
            if m == 2: ft[q, g] = rng.choice(np.array([0, 1, 7, 8, 20000, 65279, 65280, 65281, 65535]), V)
    return pack(s, r, x, nx, sr, ft)
def setup_inputs_near(rng):
    s, r, x, nx, sr, ft = parts(rng); own = np.arange(V)
    mid = 112 + (r[:, 5:7] & 15); s = s & 3; x = x & 3; r[:, ::2] = r[:, ::2] & 3; r[:, 5:7] = mid
    sr = np.where(rng.random((N, 8, V)) < 0.25, own, sr); ft = rng.integers(285, 336, (N, 8, V))
    ft[:, 5:7] = np.where(rng.random((N, 2, V)) < 0.5, 65535, ft[:, 5:7])
    return pack(s, r, x, nx, sr, ft)
def setup_inputs_rounds(rng):
    s, r, x, nx, sr, ft = parts(rng); m = V - N; e = np.arange(m); st = (3 * e) // m
    for g in range(8):
        if g in (3, 7):
            s[:, g] = s[:, g] & 3; x[:, g] = x[:, g] & 3; r[:, g] = 112 + (r[:, g] & 7); ft[:, g] = 65535
            continue
        o = rng.permutation(V); tg = o[:N]
        for q in range(N):
            row = 255 * rng.integers(0, 2, (16, 1)); kind = rng.integers(0, 3, (1, V))
            d = np.where(kind == 0, 255, np.where(kind == 1, 255 - rng.integers(0, 101, (16, V)), rng.integers(0, 128, (16, V))))
            s[q, g] = row.astype(np.uint8); x[q, g] = np.where(row == 0, d, 255 - d).astype(np.uint8)
            mid = 112 + (r[q, g] & 7); mid[:, tg[np.arange(N) != q]] = rng.integers(0, 8, (16, N - 1)) + 248 * rng.integers(0, 2, (1, N - 1)); r[q, g] = mid
            sl = rng.permutation(o[N:]); nx[q, g, tg] = tg; sr[q, g, tg] = tg; nx[q, g, sl] = tg[(q + 1 + st) % N]
            w = 1 + (q + 3 * g) % 7; c = 8 * int(rng.integers(1, 4)) + w
            later = e % (w + 1) if (q + g) % 2 == 0 else e % 10
            off = np.where(st == 0, np.where(e < c, 1 + e % 9, -(e % 9)), np.where(st == 1, later, e % 10))
            ft[q, g] = 0; ft[q, g, sl] = np.maximum(16 * np.add.reduce(d, axis=0)[sl] + off, 0)
    return pack(s, r, x, nx, sr, ft)
def check_inputs(d):
    bad = []
    for k, lo, hi in (("prof", 0, 255), ("resid", 0, 255), ("obs", 0, 255), ("nx0", 0, V - 1), ("src0", 0, V - 1), ("fit0", 0, 65535)):
        v = np.asarray(d[k]).astype(np.float64)
        if not (np.min(v) >= lo and np.max(v) <= hi): bad.append("range of " + k)
        elif np.any(v != np.floor(v)): bad.append("whole numbers of " + k)
    return bad
def reference(prof, resid, obs, nx0, src0, fit0):
    sp = np.ascontiguousarray(prof.astype(np.float32).astype(np.int16).reshape(N, 8, 16, W).transpose(0, 1, 3, 2)).reshape(N, 8 * W, 16)
    ob = np.ascontiguousarray(obs.astype(np.float32).astype(np.int16).reshape(N, 8, 16, V).transpose(0, 1, 3, 2))
    r = resid.astype(np.int64).reshape(N, 8, 16, V); ft = fit0.astype(np.int64)
    nx = np.stack([gentries(a) for a in nx0]).astype(np.int64); sr = np.stack([gentries(a) for a in src0]).astype(np.int64)
    acc = np.zeros((N, 8), np.int64); odd = 2 * np.arange(V) + 1; first = (np.arange(8) * W)[:, None, None]; site = np.arange(16)[None, :, None]; none = 2 ** 20
    def cost(a, p):
        col = ((odd * (p + 4096)) >> SH) & (W - 1)
        return np.add.reduce(np.abs(np.take(sp[a], first + col, axis=0) - ob[a][:, None]), axis=-1, dtype=np.int64)
    for t in range(RO):
        tot = np.add.reduce(r, axis=2); r2, nx2, sr2, ft2, took = [], [], [], [], []
        for a in range(N):
            q = (a + 1 + t % (N - 1)) % N; n = nx[a]
            best = np.full((8, V), none, np.int64); bn = np.zeros((8, V), np.int64); bl = r[a]
            for z in range(CH):
                if z > 0: n = np.take_along_axis(sr[q], n, 1)
                l = np.take_along_axis(r[q], n[:, None, :], 2)
                dl = (tot[a] - np.take_along_axis(tot[q], n, 1))[:, None, :]
                p = np.add.accumulate(l, axis=1); g = cost(a, p); h = cost(a, p + dl)
                sc = np.add.accumulate(g, axis=1) - g + np.add.accumulate(h[:, ::-1], axis=1)[:, ::-1]
                sc = np.where((l + dl >= 0) & (l + dl <= 255), sc, none)
                j = np.argmin(sc, axis=1); m = np.min(sc, axis=1); better = m < best
                bl = np.where(better[:, None, :], l + np.where(site == j[:, None, :], dl, 0), bl)
                bn = np.where(better, n, bn); best = np.where(better, m, best)
            ok = best < ft[a] - (acc[a] & 7)[:, None]
            r2.append(np.where(ok[:, None, :], bl, r[a])); ft2.append(np.where(ok, best, ft[a])); sr2.append(np.where(ok, bn, sr[a]))
            nx2.append(np.where(ok, (13 * bn + best) & (V - 1), n)); took.append(np.add.reduce(ok.astype(np.int64), axis=1))
        r, nx, sr, ft = np.stack(r2), np.stack(nx2), np.stack(sr2), np.stack(ft2); acc = acc + np.stack(took)
    return {"yr": r.reshape(N, 128, V).astype(np.float32), "yf": ft.astype(np.float32), "yn": nx.astype(np.float32)}

@@ -1,0 +1,539 @@
+from concourse.mybir import AluOpType as OP, AxisListType, ActivationFunctionType as AF
+
+NC = 48
+NB = 128 - NC
+CFIRST = 24
+NL = 32
+BIG = float(2 ** 26)
+
+SCRATCH = {
+    "S": ("sbuf", [128, 4096], "bfloat16"), "X": ("sbuf", [128, 256], "bfloat16"),
+    "XE": ("sbuf", [128, 16 * (128 + NB)], "bfloat16"),
+    "RI": ("sbuf", [128, 256], "int32"), "SI": ("sbuf", [128, 16], "int32"), "NI": ("sbuf", [128, 16], "int32"),
+    "FI": ("sbuf", [128, 256], "int32"), "FF": ("sbuf", [128, 512], "float32"),
+    "F": ("sbuf", [128, 16], "float32"), "FT": ("sbuf", [128, 16], "float32"),
+    "SN": ("sbuf", [128, 32], "bfloat16"),
+    "ip": ("sbuf", [128, 1], "int32"), "ic": ("sbuf", [128, 8], "int32"), "CF": ("sbuf", [128, 8], "float32"),
+    "dm": ("sbuf", [128, 128], "bfloat16"), "jm1": ("sbuf", [128, 128], "bfloat16"), "jb": ("sbuf", [128, 128], "bfloat16"),
+    "gm": ("sbuf", [128, 128], "bfloat16"), "gm2": ("sbuf", [128, 128], "bfloat16"), "jw": ("sbuf", [128, 256], "bfloat16"),
+    "JK": ("sbuf", [128, 384], "bfloat16"), "ODD0": ("sbuf", [128, 256], "float32"), "ODDB": ("sbuf", [128, 4 * NB], "float32"), "ODDC": ("sbuf", [128, 4 * NC], "float32"),
+    "IQ": ("sbuf", [128, 16], "float32"),
+    "SW": ("sbuf", [128, 512], "bfloat16"), "B": ("sbuf", [128, 128], "bfloat16"), "B32": ("sbuf", [128, 128], "bfloat16"),
+    "BX": ("sbuf", [128, 128], "bfloat16"), "JA": ("sbuf", [128, 128], "bfloat16"), "JB": ("sbuf", [128, 128], "bfloat16"),
+    "TRI": ("sbuf", [128, 128], "bfloat16"), "HN": ("sbuf", [128, 128], "bfloat16"), "I": ("sbuf", [128, 128], "bfloat16"),
+    "IB": ("sbuf", [128, 128], "bfloat16"), "NBM": ("sbuf", [128, 128], "bfloat16"), "P22": ("sbuf", [128, 128], "bfloat16"),
+    "LG": ("sbuf", [128, 15 * 128], "bfloat16"), "LH": ("sbuf", [128, 16 * 128], "bfloat16"),
+    "J16": ("sbuf", [128, 128], "bfloat16"), "ones": ("sbuf", [128, 256], "bfloat16"),
+    "KM": ("sbuf", [128, 256], "bfloat16"), "RS": ("sbuf", [128, 128], "float32"),
+    "XS": ("sbuf", [128, 256], "bfloat16"), "SR": ("sbuf", [128, 256], "bfloat16"), "NR": ("sbuf", [128, 256], "bfloat16"),
+    "D0": ("sbuf", [128, 80], "int32"), "D1": ("sbuf", [128, 80], "float32"), "FS": ("sbuf", [128, 80], "bfloat16"), "SEL": ("sbuf", [128, 16], "uint16"), "EX": ("sbuf", [128, 16], "uint16"),
+    "AI": ("sbuf", [128, 2], "int32"), "AFl": ("sbuf", [128, 2], "float32"), "AS": ("sbuf", [128, 16], "bfloat16"),
+    "AR": ("sbuf", [128, 512], "bfloat16"), "PN": ("sbuf", [128, 512], "bfloat16"),
+    "L0": ("sbuf", [128, 256], "bfloat16"), "L1": ("sbuf", [128, 256], "bfloat16"), "N1t": ("sbuf", [128, 16], "uint16"),
+    "OC": ("sbuf", [128, 4 * NC], "uint16"), "CD": ("sbuf", [128, 64 * NC], "bfloat16"),
+    "TI": ("sbuf", [128, 48], "int32"), "TF": ("sbuf", [128, 112], "float32"),
+    "IBo": ("sbuf", [128, 4 * NB], "int32"), "IC": ("sbuf", [128, 4 * NC], "int32"), "OB": ("sbuf", [128, 4 * NB], "uint16"),
+    "KA0": ("psum", [128, 512], "float32"), "KA1": ("psum", [128, 512], "float32"),
+    "KB0": ("psum", [128, 512], "float32"), "KB1": ("psum", [128, 512], "float32"),
+    "PO0": ("psum", [128, 512], "float32"), "PO1": ("psum", [128, 512], "float32"),
+    "MI1": ("psum", [128, 512], "float32"), "MI2": ("psum", [128, 512], "float32"),
+}
+for _t in range(4):
+    SCRATCH["W%d" % _t] = ("sbuf", [128, 528], "bfloat16")
+    SCRATCH["ST%d" % _t] = ("sbuf", [128, 272], "bfloat16")
+for _c in range(2):
+    SCRATCH["N0t%d" % _c] = ("sbuf", [128, 16], "uint16")
+    SCRATCH["N0q%d" % _c] = ("sbuf", [128, 16], "bfloat16")
+    SCRATCH["X1%d" % _c] = ("sbuf", [128, 256], "bfloat16")
+    SCRATCH["OA%d" % _c] = ("sbuf", [128, 256], "uint16")
+    SCRATCH["IA%d" % _c] = ("sbuf", [128, 256], "int32")
+    for _v in range(2):
+        SCRATCH["DA%d%d" % (_c, _v)] = ("sbuf", [128, 2048], "bfloat16")
+        SCRATCH["DB%d%d" % (_c, _v)] = ("sbuf", [128, 16 * NB], "bfloat16")
+    for _n in ("K0S", "km", "XT"):
+        SCRATCH[_n + str(_c)] = ("sbuf", [128, 128], "float32")
+for _n in ("OUT", "ZO", "ZR"):
+    SCRATCH[_n] = ("sbuf", [128, 256], "float32")
+SCRATCH["Y"] = ("sbuf", [128, 256], "int32")
+for _n in ("CR", "CT", "OH", "BS", "MD"):
+    SCRATCH[_n] = ("sbuf", [128, 256], "bfloat16")
+SCRATCH["ZC"] = ("sbuf", [128, 256], "int32")
+
+NDMA = 16
+SEMAPHORES = ["sV", "sA", "sP", "sG", "sL"] + ["d%d" % k for k in range(NDMA)] + ["arr%d" % k for k in range(4)]
+PSUM = ("KA0", "KA1", "KB0", "KB1", "PO0", "PO1", "MI1", "MI2")
+
+
+def rank_program(g, core, T, topo):
+    rank = T.rank_of(core)
+    if rank is None:
+        return
+    NR_ = len(T.cores)
+    queues = {"V": g.vector, "A": g.scalar, "P": g.tensor, "G": g, "S": g.sync}
+
+    ops, last, ndma, sent, compn = [], {}, [0], [0], {}
+
+    def norm(x):
+        if isinstance(x, str):
+            return (x, 0, 1 << 30)
+        return x
+
+    def op(q, fn, r=(), w=(), comp=None, amt=1):
+        me = len(ops)
+        deps = set()
+        rr, ww = [norm(x) for x in r], [norm(x) for x in w]
+        for name, a, b in rr:
+            for (a2, b2, o, iw) in last.get(name, []):
+                if name in PSUM:
+                    if ops[o]["q"] != q:
+                        deps.add(o)
+                elif iw and a < b2 and a2 < b:
+                    deps.add(o)
+        for name, a, b in ww:
+            for (a2, b2, o, iw) in last.get(name, []):
+                if name in PSUM:
+                    if ops[o]["q"] != q or q != "P":
+                        deps.add(o)
+                elif a < b2 and a2 < b:
+                    deps.add(o)
+        for name, a, b in ww:
+            ps = name in PSUM
+            last[name] = [e for e in last.get(name, []) if not (ps or (a <= e[0] and e[1] <= b))] + [(a, b, me, True)]
+        for name, a, b in rr:
+            last.setdefault(name, []).append((a, b, me, False))
+        comp = comp or q
+        ci = compn.get(comp, 0)
+        compn[comp] = ci + 1
+        deps.discard(me)
+        ops.append({"q": q, "fn": fn, "deps": deps, "comp": comp, "ci": ci, "amt": amt, "sig": amt != 1, "need": []})
+
+    def dma(q, out, in_, r=(), w=()):
+        k = ndma[0]
+        ndma[0] += 1
+        qq = queues[q]
+        op(q, lambda: qq.dma_start(out, in_), r, w, "d%d" % k, 16)
+
+    def V(name, r, w, *a, **k):
+        fn = {"tt": g.vector.tensor_tensor, "ts": g.vector.tensor_scalar, "cp": g.vector.tensor_copy, "tr": g.vector.transpose,
+              "scan": g.vector.tensor_tensor_scan, "set": g.vector.memset}[name]
+        op("V", lambda: fn(*a, **k), r, w)
+
+    def A(r, w, out, in_, func, **k):
+        op("A", lambda: g.scalar.activation(out, in_, func, **k), r, w)
+
+    def mm(r, w, out, lhsT, rhs, start, stop):
+        op("P", lambda: g.tensor.matmul(out, lhsT, rhs, start, stop), r, w)
+
+    def iota(w, out, pattern, base, cm, small=True):
+        if small:
+            op("G", lambda: g.iota(out, pattern, base, cm, allow_small_or_imprecise_dtypes=True), (), w)
+        else:
+            op("G", lambda: g.iota(out, pattern, base, cm), (), w)
+
+    def swap(bank, ap, r):
+        for y in range(2):
+            for x in range(2):
+                mm(["SW"] + r, [bank], T[bank][:, y:16:2], T.SW[:, 128 * (2 * y + x):128 * (2 * y + x) + 128], ap(x), x == 0, x == 1)
+
+    def send(t, dst):
+        rid, pid, _ = topo.addr(dst)
+        m = topo.mask(core, dst)
+        sent[0] += len(topo.engines(core, dst))
+        out, src = T["W%d" % t][:, 256:528], T["ST%d" % t][:]
+        op("G", lambda: g.remote_dma(out, src, T.sem["arr%d" % t], T.sem.sL, pid, rid, m), ["ST%d" % t], (), "sL", 0)
+
+    def recv(t, src):
+        op("N", None, (), [("W%d" % t, 256, 528)], "arr%d" % t, len(topo.engines(src, core)))
+
+    dma("S", T.RI[:], T.resid[:], (), ["RI"])
+    dma("A", T.SI[:], T.src0[:], (), ["SI"])
+    dma("S", T.NI[:], T.nx0[:], (), ["NI"])
+    dma("A", T.X[:], T.obs[:], (), ["X"])
+    dma("S", T.S[:, 0:2048], T.prof[:, 0:2048], (), [("S", 0, 2048)])
+    dma("A", T.S[:, 2048:4096], T.prof[:, 2048:4096], (), [("S", 2048, 4096)])
+
+    iota(["ip"], T.ip[:], [[0, 1]], 0, 1, False)
+    iota(["dm"], T.dm[:], [[1, 128]], 0, -1)
+    V("set", (), ["FI"], T.FI[:], 0)
+    dma("S", T.FI[0:128:16, :], T.fit0[:], (), ["FI"])
+    iota(["gm"], T.gm[:], [[1, 8], [0, 16]], 0, 0)
+    iota(["jm1"], T.jm1[:], [[0, 8], [1, 16]], 1, 0)
+    iota(["jb"], T.jb[:], [[0, 8], [1, 16]], -20, 0)
+    iota(["jw"], T.jw[:], [[0, 16], [1, 16]], 0, 0)
+    V("ts", ["ip"], [("ic", 0, 1)], T.ic[:, 0:1], T.ip[:], 15, None, OP.bitwise_and)
+    V("ts", ["ip"], [("ic", 1, 2)], T.ic[:, 1:2], T.ip[:], 4, None, OP.arith_shift_right)
+    V("ts", ["ip"], [("ic", 2, 3)], T.ic[:, 2:3], T.ip[:], 4, 1, OP.arith_shift_right, OP.bitwise_and)
+    V("ts", ["ip"], [("ic", 3, 4)], T.ic[:, 3:4], T.ip[:], 31, None, OP.bitwise_and)
+    V("ts", ["ip"], [("ic", 4, 5)], T.ic[:, 4:5], T.ip[:], 5, None, OP.arith_shift_right)
+
+    def col(k, s, m, a):
+        V("ts", [("ic", s, s + 1)], [("CF", k, k + 1)], T.CF[:, k:k + 1], T.ic[:, s:s + 1], float(m), float(a), OP.mult, OP.add)
+
+    def C(k):
+        return T.CF[:, k:k + 1]
+    col(3, 2, 1, 0)
+    col(4, 2, -1, 1)
+    col(0, 0, 1, 1)
+    col(1, 0, 1, -20)
+    col(2, 1, 1, 0)
+    col(5, 0, 1, 0)
+    col(6, 3, 1, 0)
+    col(7, 4, 1, 0)
+    for y in range(2):
+        for x in range(2):
+            s = 128 * (2 * y + x)
+            V("ts", ["dm", ("CF", 3, 5)], [("SW", s, s + 128)], T.SW[:, s:s + 128], T.dm[:], float(16 * (x - y)), C(3 if y else 4),
+              OP.is_equal, OP.mult)
+    V("cp", ["SI"], [("SN", 0, 16)], T.SN[:, 0:16], T.SI[:])
+    V("cp", ["NI"], [("SN", 16, 32)], T.SN[:, 16:32], T.NI[:])
+    V("cp", ["NI"], ["N0t0"], T.N0t0[:], T.NI[:])
+    V("cp", ["RI"], [("ST0", 0, 256)], T.ST0[:, 0:256], T.RI[:])
+    swap("MI1", lambda x: T.SN[:, x:16:2], [("SN", 0, 16)])
+    V("cp", ["MI1"], [("ST0", 256, 272)], T.ST0[:, 256:272], T.MI1[:, 0:16])
+    send(0, T.cores[(rank - 1) % NR_])
+    swap("MI2", lambda x: T.SN[:, 16 + x:32:2], [("SN", 16, 32)])
+    V("cp", ["MI2"], ["N0q0"], T.N0q0[:], T.MI2[:, 0:16])
+    iota(["ODD0"], T.ODD0[:], [[0, 2], [2, 128]], 1, 0)
+    NX = 128 + NB
+    for k in range(16):
+        A(["X"], [("XEk", k, k + 1)], T.XE[:, k:16 * NX:16], T.X[:, 0:NX], AF.Copy)
+    V("set", (), ["ones"], T.ones[:], 1.0)
+    V("set", (), [("JK", 256, 384)], T.JK[0:1, 256:384], 4096.0)
+    V("set", (), ["J16"], T.J16[0:1, :], 16.0)
+    V("cp", ["jw"], ["EX"], T.EX[:], T.jw[:, 0:16])
+    V("ts", ["jw"], ["KM"], T.KM[:], T.jw[:], 0.0, None, OP.is_gt)
+    V("ts", ["gm", "CF"], ["B"], T.B[:], T.gm[:], C(2), None, OP.is_equal)
+    V("ts", ["B"], ["BX"], T.BX[:], T.B[:], 32.0, None, OP.mult)
+    V("tt", ["jm1", "B"], ["JA"], T.JA[:], T.jm1[:], T.B[:], OP.mult)
+    V("tt", ["jb", "B"], ["JB"], T.JB[:], T.jb[:], T.B[:], OP.mult)
+    V("ts", ["JA", "CF"], ["TRI"], T.TRI[:], T.JA[:], C(0), None, OP.is_ge)
+    V("ts", ["JB", "CF"], ["HN"], T.HN[:], T.JB[:], C(1), -1.0, OP.is_lt, OP.mult)
+    V("ts", ["JA", "CF"], ["I"], T.I[:], T.JA[:], C(0), None, OP.is_equal)
+    V("tt", ["I", "B"], ["IB"], T.IB[:], T.I[:], T.B[:], OP.subtract)
+    V("ts", ["B"], ["NBM"], T.NBM[:], T.B[:], -1.0, None, OP.mult)
+    V("ts", ["I"], ["P22"], T.P22[:], T.I[:], float(2 ** 22), None, OP.mult)
+    V("ts", ["jw"], ["RS"], T.RS[:], T.jw[:, 0:128], 0.0, BIG, OP.is_equal, OP.mult)
+    for k in range(4):
+        V("ts", ["JA"], [("LG", k, k + 1)], T.LG[:, 128 * k:128 * k + 128], T.JA[:], float(k + 1), 32.0, OP.is_gt, OP.mult)
+
+    def step(name, k, base, m):
+        out = T[name][:, 128 * k:128 * k + 128]
+        op("G", lambda: g.affine_select(out, T.BX[:], [[0, 8], [m, 16]], OP.is_ge, 0.0, base, 0), ["BX"], [(name, k, k + 1)])
+    for k in range(4, 15):
+        step("LG", k, -k - 1, 1)
+    iota(["ODDC"], T.ODDC[:], [[2, NC], [0, 4]], 257 + 2 * NB, 0)
+    iota([("JK", 0, 256)], T.JK[0:1, 0:256], [[16, 2], [0, 8], [1, 16]], 0, 0)
+    for k in range(16):
+        step("LH", k, k, -1)
+    iota(["ODDB"], T.ODDB[:], [[0, 4], [2, NB]], 257, 0)
+    iota(["IQ"], T.IQ[:], [[32, 8], [0, 2]], -256, 0)
+    iota(["gm2"], T.gm2[:], [[1, 4], [0, 32]], 0, 0)
+
+    def lastconsts():
+        V("cp", ["FI"], [("FF", 0, 256)], T.FF[:, 0:256], T.FI[:])
+        V("tr", [("FF", 0, 256)], [("FF", 256, 512)], T.FF[:, 256:512], T.FF[:, 0:256])
+        V("cp", [("FF", 256, 512)], ["F"], T.F[:], T.FF[:, 256:512:16])
+        V("ts", ["F"], ["FT"], T.FT[:], T.F[:], 32.0, None, OP.mult)
+        V("ts", ["IQ", "CF"], ["IQ"], T.IQ[:], T.IQ[:], C(6), None, OP.add)
+        V("ts", ["gm2", "CF"], ["B32"], T.B32[:], T.gm2[:], C(7), None, OP.is_equal)
+        V("set", (), ["AS"], T.AS[:], 0.0)
+        V("set", (), ["ZC"], T.ZC[:], 0)
+        V("set", (), ["D0"], T.D0[:], 0)
+        for k in (1, 3):
+            V("ts", ["IQ"], [("D0", k, k + 1)], T.D0[:, k:80:5], T.IQ[:], 0.0, 1.0, OP.mult, OP.add)
+        V("ts", ["IQ"], [("D1", 3, 4)], T.D1[:, 3:80:5], T.IQ[:], -1.0, None, OP.mult)
+        V("cp", ["IQ"], [("D1", 4, 5)], T.D1[:, 4:80:5], T.IQ[:])
+        V("set", (), ["ZO"], T.ZO[:], 0.0)
+
+    for t in range(4):
+        par = t & 1
+        W, Wn = T["W%d" % t], "W%d" % t
+        ST, STn = T["ST%d" % t], "ST%d" % t
+        n0t, n0q, x1 = "N0t%d" % par, "N0q%d" % par, "X1%d" % par
+        m0, mt = "N0q%d" % (1 - par), "N0t%d" % (1 - par)
+        n1q = T[x1][:, 0:256:16]
+        recv(t, T.cores[(rank + 1 + t % (NR_ - 1)) % NR_])
+
+        def pos0(v, bank, a, b, o):
+            mm([("JK", 256, 384), "ones"], [bank], o, T.JK[0:1, 256:384], T.ones[0:1, 0:b - a], True, False)
+            if v:
+                mm(["B", ("ST0", 0, 256)], [bank], o, T.B[:], T.ST0[:, a:b], False, False)
+
+        def pos1(c, v, bank, a, b, o):
+            m = "HN" if v else "TRI"
+            mm([m, ("L%d" % c, a, b)], [bank], o, T[m][:], T["L%d" % c][:, a:b], False, True)
+
+        def pos(c, v, bank, a, b, o):
+            pos0(v, bank, a, b, o)
+            pos1(c, v, bank, a, b, o)
+
+        def allowed(c):
+            mm(["B", ("ST0", 0, 256)], ["MI1"], T.MI1[:, 0:256], T.B[:], T.ST0[:, 0:256], True, False)
+            mm(["IB", "L%d" % c], ["MI1"], T.MI1[:, 0:256], T.IB[:], T["L%d" % c][:, 0:256], False, True)
+            A(["MI1"], [("AR", c, c + 1)], T.AR[:, 256 * c:256 * c + 256], T.MI1[:, 0:256], AF.Abs, bias=-127.5)
+
+        def offsets(bank, odd, o, a, b):
+            In = "IBo" if o == "OB" else "I" + o[1:]
+            ib = T[In][:, a:b]
+            V("tt", [bank, odd], [(In, a, b)], ib, T[bank][:, 0:b - a], T[odd][:, 0:b - a], OP.mult)
+            V("ts", [(In, a, b)], [(In, a, b)], ib, ib, 2, 4095, OP.arith_shift_right, OP.bitwise_and)
+            V("cp", [(In, a, b)], [(o, a, b)], T[o][:, a:b], ib)
+
+        def gat(c, v, s, n0=0, n1=None):
+            d = "D%s%d%d" % (s, c, v)
+            o, k = ("OA%d" % c, 128 * v) if s == "A" else ("OB", NB * (2 * c + v))
+            n1 = (128 if s == "A" else NB) if n1 is None else n1
+            xb = 0 if s == "A" else 2048
+            V("tt", ["S", "XEk", (o, k + n0, k + n1)], [(d, 16 * n0, 16 * n1)], T[d][:, 16 * n0:16 * n1],
+              T.S[:, 0:4096].indirect(T[o][:, k + n0:k + n1]), T.XE[:, xb + 16 * n0:xb + 16 * n1], OP.subtract)
+
+        def absv(c, v, s, n0=0, n1=None):
+            d = "D%s%d%d" % (s, c, v)
+            n1 = (128 if s == "A" else NB) if n1 is None else n1
+            A([(d, 16 * n0, 16 * n1)], [(d, 16 * n0, 16 * n1)], T[d][:, 16 * n0:16 * n1], T[d][:, 16 * n0:16 * n1], AF.Abs)
+
+        def keystart(c, bank, a, b, sl):
+            mm([("JK", 0, 256), "ones"], [bank], T[bank][:, a:b], T.JK[0:1, 128 * c:128 * c + 128], T.ones[0:1, 0:b - a], True, False)
+            mm(["P22", "PN"], [bank], T[bank][:, a:b], T.P22[:], T.PN[:, 256 * c + sl:256 * c + sl + b - a], False, False)
+
+        def keys(c, v, s, bank):
+            d = "D%s%d%d" % (s, c, v)
+            n = 128 if s == "A" else NB
+            if v == 0:
+                keystart(c, bank, 0, n, 0 if s == "A" else 128)
+            for k in range(15 + v):
+                l = "LH" if v else "LG"
+                mm([(l, k, k + 1), d], [bank], T[bank][:, 0:n], T[l][:, 128 * k:128 * k + 128], T[d][:, k:16 * n:16], False, v == 1 and k == 15)
+
+        def cslots(a, b):
+            for s in range(a, b):
+                i = 256 - NC + s
+                A(["S", "OC", "X"], [("CD", s, s + 1)], T.CD[:, 64 * s:64 * s + 64], T.S[:, 0:4096].indirect(T.OC[:, 4 * s:4 * s + 4]), AF.Abs,
+                  bias=T.X[:, i:i + 1], scale=-1.0)
+
+        def keysc(s0, s1):
+            n, o = s1 - s0, T.KB0[:, 256 + 2 * s0:256 + 2 * s1]
+            mm([("JK", 0, 256), "ones"], ["KB0"], o, T.JK[0:1, 0:128], T.ones[0:1, 0:2 * n], True, False)
+            mm(["J16", "ones"], ["KB0"], T.KB0[:, 257 + 2 * s0:256 + 2 * s1:2], T.J16[0:1, :], T.ones[0:1, 0:n], False, False)
+            for c in range(2):
+                i = 256 * c + 256 - NC
+                mm(["P22", "PN"], ["KB0"], T.KB0[:, 256 + 2 * s0 + c:256 + 2 * s1:2], T.P22[:], T.PN[:, i + s0:i + s1], False, False)
+            for v in range(2):
+                l = "LH" if v else "LG"
+                for k in range(15 + v):
+                    mm([(l, k, k + 1), ("CD", s0, s1)], ["KB0"], o, T[l][:, 128 * k:128 * k + 128],
+                       T.CD[:, 64 * s0 + 16 * v + k:64 * s1:32], False, v == 1 and k == 15)
+
+        def I_(k):
+            return T.TI[:, 16 * k:16 * k + 16]
+
+        def F_(k):
+            return T.TF[:, 16 * k:16 * k + 16]
+
+        def ri(k):
+            return ("TI", k, k + 1)
+
+        def rf(k):
+            return ("TF", k, k + 1)
+        key, acc, nsel = T.Y[:, 15:256:16], T.D0[:, 4:80:5], T.FS[:, 2:80:5]
+
+        def n0steps(n, r):
+            V("ts", r, [("D1", 1, 2)], T.D1[:, 1:80:5], n, -1.0, None, OP.mult)
+            V("cp", r, [("D1", 2, 3)], T.D1[:, 2:80:5], n)
+
+        def best(h):
+            x, a, b = str(h), 128 * h, 128 * h + 128
+            k1 = "KA1" if h == 0 else "KB1"
+            n = 128 if h == 0 else NB
+            V("tt", [k1, ("K0S" + x, 0, n)], [("km" + x, 0, n)], T["km" + x][:, 0:n], T[k1][:, 0:n], T["K0S" + x][:, 0:n], OP.min)
+            V("tr", ["km" + x], ["XT" + x], T["XT" + x][:], T["km" + x][:])
+            V("scan", ["RS", "XT" + x], [("Y", a, b)], T.Y[:, a:b], T.RS[:], T["XT" + x][:], BIG, OP.add, OP.min)
+
+        def site(h, part):
+            a, b = 128 * h, 128 * h + 128
+            if part == 0:
+                V("ts", [("Y", a, b)], [("ZC", a, b)], T.ZC[:, a:b:16], T.Y[:, a + 15:b:16], 15, None, OP.bitwise_and)
+                V("scan", ["KM", ("ZC", a, b)], [("CR", a, b)], T.CR[:, a:b], T.KM[:, a:b], T.ZC[:, a:b], 0.0, OP.mult, OP.add)
+                V("tr", [("CR", a, b)], [("CT", a, b)], T.CT[:, a:b], T.CR[:, a:b])
+            else:
+                V("ts", [("CT", a, b), "CF"], [("OH", a, b)], T.OH[:, a:b], T.CT[:, a:b], C(5), None, OP.is_equal)
+
+        def accept():
+            V("ts", ["Y"], [("D0", 2, 3)], T.D0[:, 2:80:5], key, 4, 1, OP.arith_shift_right, OP.bitwise_and)
+            V("tt", ["Y", "FT"], [("D0", 4, 5)], acc, key, T.FT[:], OP.is_lt)
+            V("scan", ["D0", "D1"], ["FS"], T.FS[:], T.D0[:], T.D1[:], 0.0, OP.mult, OP.add)
+            swap("MI2", lambda x: T.FS[:, 4 + 5 * x:80:10], ["FS"])
+            site(1, 0)
+            V("ts", ["MI2"], ["SEL"], T.SEL[:], T.MI2[:, 0:16], 256.0, None, OP.add)
+            mm(["B", ("ST0", 0, 256)], ["MI1"], T.MI1[:, 0:256], T.B[:], T.ST0[:, 0:256], True, False)
+            V("cp", [(Wn, 0, 512), "SEL"], ["BS"], T.BS[:], W[:, 0:512].indirect(T.SEL[:, 0:16]))
+            mm(["NBM", "BS"], ["MI1"], T.MI1[:, 0:256], T.NBM[:], T.BS[:], False, True)
+            mm(["I", "BS"], ["MI2"], T.MI2[:, 0:256], T.I[:], T.BS[:], True, True)
+            site(1, 1)
+
+        def newlists(out, w):
+            V("tt", ["MI1", "OH"], ["MD"], T.MD[:], T.MI1[:, 0:256], T.OH[:], OP.mult)
+            V("tt", ["MI2", "MD"], w, out, T.MI2[:, 0:256], T.MD[:], OP.add)
+
+        def newsrc():
+            sn = "ST%d" % (t + 1)
+            so, wo = ST[:, 256:272], (STn, 256, 272)
+            V("tt", ["FS", wo], [rf(0)], F_(0), nsel, so, OP.subtract)
+            V("tt", [rf(0), ("D0", 4, 5)], [rf(1)], F_(1), F_(0), acc, OP.mult)
+            V("tt", [rf(1), wo], [(sn, 256, 272)], T[sn][:, 256:272], F_(1), so, OP.add)
+
+        def newnx(out, w):
+            V("ts", ["FS"], [rf(2)], F_(2), nsel, 416.0, None, OP.mult)
+            V("tt", [rf(2), "Y"], [ri(0)], I_(0), F_(2), key, OP.add)
+            V("ts", [ri(0)], [ri(1)], I_(1), I_(0), 5, 255, OP.arith_shift_right, OP.bitwise_and)
+            V("tt", [ri(1), x1], [rf(3)], F_(3), I_(1), n1q, OP.subtract)
+            V("tt", [rf(3), ("D0", 4, 5)], [rf(4)], F_(4), F_(3), acc, OP.mult)
+            V("tt", [rf(4), x1], w, out, F_(4), n1q, OP.add)
+
+        def newf(out, w):
+            V("ts", ["Y"], [ri(2)], I_(2), key, 5, None, OP.arith_shift_right)
+            V("tt", [ri(2), "F"], [rf(5)], F_(5), I_(2), T.F[:], OP.subtract)
+            V("tt", [rf(5), ("D0", 4, 5)], [rf(6)], F_(6), F_(5), acc, OP.mult)
+            V("tt", [rf(6), "F"], w, out, F_(6), T.F[:], OP.add)
+
+        PW = (Wn, 256, 512)
+        V("cp", [PW, n0t], [("L0", 0, 128)], T.L0[:, 0:128], W[:, 256:512].indirect(T[n0t][:, 0:8]))
+        A([(Wn, 512, 528), "EX"], ["XS"], T.XS[:], W[:, 512:528].indirect(T.EX[:, 0:16]), AF.Copy)
+        oA = T.PO0[:, 0:128]
+        pos0(0, "PO0", 0, 128, oA)
+        pos0(1, "PO1", 0, 128, T.PO1[:, 0:128])
+        pos1(0, 0, "PO0", 0, 128, oA)
+        pos1(0, 1, "PO1", 0, 128, T.PO1[:, 0:128])
+        V("tr", ["XS"], ["SR"], T.SR[:], T.XS[:])
+        A(["SR", n0t], ["NR"], T.NR[:], T.SR[:, 0:256].indirect(T[n0t][:, 0:16]), AF.Copy)
+        A([PW, n0t], [("L0", 128, 256)], T.L0[:, 128:256], W[:, 256:512].indirect(T[n0t][:, 8:16]), AF.Copy)
+        offsets("PO0", "ODD0", "OA0", 0, 128)
+        V("tr", ["NR"], [x1], T[x1][:], T.NR[:])
+        gat(0, 0, "A", 0, 64)
+        swap("MI2", lambda x: T[x1][:, 16 * x:256:32], [x1])
+        if t == 0:
+            A([(STn, 0, 256)], [(Wn, 0, 256)], W[:, 0:256], ST[:, 0:256], AF.Copy)
+        V("cp", ["MI2"], ["N1t"], T.N1t[:], T.MI2[:, 0:16])
+        offsets("PO1", "ODD0", "OA0", 128, 256)
+        A([PW, "N1t"], ["L1"], T.L1[:], W[:, 256:512].indirect(T.N1t[:, 0:16]), AF.Copy)
+        absv(0, 0, "A", 0, 64)
+        for c in range(2):
+            for v in range(2):
+                pos(c, v, "PO0", 256 - NC, 256, T.PO0[:, 2 * c + v:4 * NC:4])
+        allowed(0)
+        gat(0, 0, "A", 64, 128)
+        offsets("PO0", "ODDC", "OC", 0, 4 * NC)
+        allowed(1)
+        absv(0, 0, "A", 64, 128)
+        for v in range(2):
+            pos(1, v, "PO1", 0, 128, T.PO1[:, 128 * v:128 * v + 128])
+        for c in range(2):
+            for v in range(2):
+                pos(c, v, "PO0", 128, 128 + NB, T.PO0[:, NB * (2 * c + v):NB * (2 * c + v) + NB])
+        V("ts", ["AR"], ["PN"], T.PN[:], T.AR[:], 127.5, None, OP.is_gt)
+        keys(0, 0, "A", "KA0")
+        cslots(0, CFIRST)
+        keysc(0, CFIRST)
+        gat(0, 1, "A")
+        absv(0, 1, "A")
+        keys(0, 1, "A", "KA0")
+        offsets("PO1", "ODD0", "OA1", 0, 256)
+        cslots(CFIRST, NC)
+        keysc(CFIRST, NC)
+        gat(1, 0, "A")
+        absv(1, 0, "A")
+        keys(1, 0, "A", "KA1")
+        A(["KA0"], ["K0S0"], T.K0S0[:], T.KA0[:, 0:128], AF.Copy)
+        gat(1, 1, "A")
+        offsets("PO0", "ODDB", "OB", 0, 4 * NB)
+        absv(1, 1, "A")
+        A([x1], [("D1", 0, 1)], T.D1[:, 0:80:5], n1q, AF.Copy)
+        keys(1, 1, "A", "KA1")
+        for v in range(2):
+            gat(0, v, "B")
+            absv(0, v, "B")
+            keys(0, v, "B", "KB0")
+        gat(1, 0, "B")
+        absv(1, 0, "B")
+        keys(1, 0, "B", "KB1")
+        gat(1, 1, "B", 0, NB - NL)
+        absv(1, 1, "B", 0, NB - NL)
+        gat(1, 1, "B", NB - NL, NB)
+        absv(1, 1, "B", NB - NL, NB)
+        A(["KB0"], [("K0S1", NB, 128)], T.K0S1[:, NB:128], T.KB0[:, 256:256 + 2 * NC:2], AF.Copy)
+        A(["KB0"], [("K0S1", 0, NB)], T.K0S1[:, 0:NB], T.KB0[:, 0:NB], AF.Copy)
+        keys(1, 1, "B", "KB1")
+        if t == 0:
+            lastconsts()
+            n0steps(T[n0q][:], [n0q])
+        best(0)
+        V("tt", ["KB0", ("K0S1", NB, 128)], [("km1", NB, 128)], T.km1[:, NB:128], T.KB0[:, 257:256 + 2 * NC:2], T.K0S1[:, NB:128], OP.min)
+        site(0, 0)
+        site(0, 1)
+        best(1)
+        accept()
+        if t < 3:
+            sn = "ST%d" % (t + 1)
+            newsrc()
+            newlists(T[sn][:, 0:256], [(sn, 0, 256)])
+            wn = "W%d" % (t + 1)
+            A([(sn, 0, 256)], [(wn, 0, 256)], T[wn][:, 0:256], T[sn][:, 0:256], AF.Copy)
+            send(t + 1, T.cores[(rank - 1 - (t + 1) % (NR_ - 1)) % NR_])
+            newnx(T[m0][:], [m0])
+            swap("MI1", lambda x: T[m0][:, x:16:2], [m0])
+            newf(T.F[:], ["F"])
+            V("tt", [("D0", 4, 5), "AS"], ["AS"], T.AS[:], acc, T.AS[:], OP.add)
+            for b in range(8):
+                mm(["B32", "AS"], ["MI2"], T.MI2[:, 0:2], T.B32[:], T.AS[:, 2 * b:2 * b + 2], b == 0, b == 7)
+            V("cp", ["MI1"], [mt], T[mt][:], T.MI1[:, 0:16])
+            n0steps(T[m0][:], [m0])
+            V("cp", ["MI2"], ["AI"], T.AI[:], T.MI2[:, 0:2])
+            V("ts", ["AI"], ["AI"], T.AI[:], T.AI[:], 7, None, OP.bitwise_and)
+            V("cp", ["AI"], ["AFl"], T.AFl[:], T.AI[:])
+            for x in range(2):
+                V("ts", ["AFl", "F"], [("FT", x, x + 1)], T.FT[:, x:16:2], T.F[:, x:16:2], T.AFl[:, x:x + 1], 32.0, OP.subtract, OP.mult)
+        else:
+            newnx(T.ZO[:, 1:256:16], [("ZO", 1, 2)])
+            newf(T.ZO[:, 0:256:16], [("ZO", 0, 1)])
+            newlists(T.OUT[:], ["OUT"])
+            dma("S", T.yr[:], T.OUT[:], ["OUT"], ())
+            V("tr", ["ZO"], ["ZR"], T.ZR[:], T.ZO[:])
+            dma("A", T.yf[:], T.ZR[0:128:16, :], ["ZR"], ())
+            dma("S", T.yn[:], T.ZR[1:128:16, :], ["ZR"], ())
+
+    known = {}
+    for o in ops:
+        kn = known.setdefault(o["q"], {}) if o["q"] != "N" else {}
+        for d in sorted(o["deps"], reverse=True):
+            p = ops[d]
+            if kn.get(p["comp"], -1) >= p["ci"]:
+                continue
+            o["need"].append(d)
+            p["sig"] = True
+            for c, v in p["clock"].items():
+                if kn.get(c, -1) < v:
+                    kn[c] = v
+            kn[p["comp"]] = max(kn.get(p["comp"], -1), p["ci"])
+        o["clock"] = dict(kn)
+    names = {"V": "sV", "A": "sA", "P": "sP", "G": "sG"}
+    count = {}
+    for o in ops:
+        c = names.get(o["comp"], o["comp"])
+        q = queues.get(o["q"])
+        for d in o["need"]:
+            p = ops[d]
+            q.wait_ge(T.sem[names.get(p["comp"], p["comp"])], p["val"])
+        if o["q"] == "N":
+            count[c] = count.get(c, 0) + o["amt"]
+            o["val"] = count[c]
+            continue
+        ins = o["fn"]()
+        if o["comp"] == "sL":
+            continue
+        if o["sig"]:
+            count[c] = count.get(c, 0) + o["amt"]
+            o["val"] = count[c]
+            ins.then_inc(T.sem[c], o["amt"])
+    for c in count:
+        g.wait_ge(T.sem[c], count[c])
+    g.wait_ge(T.sem.sL, sent[0])

@@ -1,67 +1,47 @@
-from concourse.mybir import AluOpType as OP, AxisListType, ActivationFunctionType as AF
+from concourse.mybir import AluOpType as OP, ActivationFunctionType as AF
 
-NC = 48
-NB = 128 - NC
-CFIRST = 24
-NL = 32
+NV = 72
+NC = 128 - NV
+GA, GB, GC = 24, 32, 44
+G0, G2, G3 = 14, 26, 32
+A1, A2, CB, A4, A5 = 5, 17, 28, 44, 54
 BIG = float(2 ** 26)
+BF, F32, I32, U16 = "bfloat16", "float32", "int32", "uint16"
 
-SCRATCH = {
-    "S": ("sbuf", [128, 4096], "bfloat16"), "X": ("sbuf", [128, 256], "bfloat16"),
-    "XE": ("sbuf", [128, 16 * (128 + NB)], "bfloat16"),
-    "RI": ("sbuf", [128, 256], "int32"), "SI": ("sbuf", [128, 16], "int32"), "NI": ("sbuf", [128, 16], "int32"),
-    "FI": ("sbuf", [128, 256], "int32"), "FF": ("sbuf", [128, 512], "float32"),
-    "F": ("sbuf", [128, 16], "float32"), "FT": ("sbuf", [128, 16], "float32"),
-    "SN": ("sbuf", [128, 32], "bfloat16"),
-    "ip": ("sbuf", [128, 1], "int32"), "ic": ("sbuf", [128, 8], "int32"), "CF": ("sbuf", [128, 8], "float32"),
-    "dm": ("sbuf", [128, 128], "bfloat16"), "jm1": ("sbuf", [128, 128], "bfloat16"), "jb": ("sbuf", [128, 128], "bfloat16"),
-    "gm": ("sbuf", [128, 128], "bfloat16"), "gm2": ("sbuf", [128, 128], "bfloat16"), "jw": ("sbuf", [128, 256], "bfloat16"),
-    "JK": ("sbuf", [128, 384], "bfloat16"), "ODD0": ("sbuf", [128, 256], "float32"), "ODDB": ("sbuf", [128, 4 * NB], "float32"), "ODDC": ("sbuf", [128, 4 * NC], "float32"),
-    "IQ": ("sbuf", [128, 16], "float32"),
-    "SW": ("sbuf", [128, 512], "bfloat16"), "B": ("sbuf", [128, 128], "bfloat16"), "B32": ("sbuf", [128, 128], "bfloat16"),
-    "BX": ("sbuf", [128, 128], "bfloat16"), "JA": ("sbuf", [128, 128], "bfloat16"), "JB": ("sbuf", [128, 128], "bfloat16"),
-    "TRI": ("sbuf", [128, 128], "bfloat16"), "HN": ("sbuf", [128, 128], "bfloat16"), "I": ("sbuf", [128, 128], "bfloat16"),
-    "IB": ("sbuf", [128, 128], "bfloat16"), "NBM": ("sbuf", [128, 128], "bfloat16"), "P22": ("sbuf", [128, 128], "bfloat16"),
-    "LG": ("sbuf", [128, 15 * 128], "bfloat16"), "LH": ("sbuf", [128, 16 * 128], "bfloat16"),
-    "J16": ("sbuf", [128, 128], "bfloat16"), "ones": ("sbuf", [128, 256], "bfloat16"),
-    "KM": ("sbuf", [128, 256], "bfloat16"), "RS": ("sbuf", [128, 128], "float32"),
-    "XS": ("sbuf", [128, 256], "bfloat16"), "SR": ("sbuf", [128, 256], "bfloat16"), "NR": ("sbuf", [128, 256], "bfloat16"),
-    "D0": ("sbuf", [128, 80], "int32"), "D1": ("sbuf", [128, 80], "float32"), "FS": ("sbuf", [128, 80], "bfloat16"), "SEL": ("sbuf", [128, 16], "uint16"), "EX": ("sbuf", [128, 16], "uint16"),
-    "AI": ("sbuf", [128, 2], "int32"), "AFl": ("sbuf", [128, 2], "float32"), "AS": ("sbuf", [128, 16], "bfloat16"),
-    "AR": ("sbuf", [128, 512], "bfloat16"), "PN": ("sbuf", [128, 512], "bfloat16"),
-    "L0": ("sbuf", [128, 256], "bfloat16"), "L1": ("sbuf", [128, 256], "bfloat16"), "N1t": ("sbuf", [128, 16], "uint16"),
-    "OC": ("sbuf", [128, 4 * NC], "uint16"), "CD": ("sbuf", [128, 64 * NC], "bfloat16"),
-    "TI": ("sbuf", [128, 48], "int32"), "TF": ("sbuf", [128, 112], "float32"),
-    "IBo": ("sbuf", [128, 4 * NB], "int32"), "IC": ("sbuf", [128, 4 * NC], "int32"), "OB": ("sbuf", [128, 4 * NB], "uint16"),
-    "KA0": ("psum", [128, 512], "float32"), "KA1": ("psum", [128, 512], "float32"),
-    "KB0": ("psum", [128, 512], "float32"), "KB1": ("psum", [128, 512], "float32"),
-    "PO0": ("psum", [128, 512], "float32"), "PO1": ("psum", [128, 512], "float32"),
-    "MI1": ("psum", [128, 512], "float32"), "MI2": ("psum", [128, 512], "float32"),
-}
-for _t in range(4):
-    SCRATCH["W%d" % _t] = ("sbuf", [128, 528], "bfloat16")
-    SCRATCH["ST%d" % _t] = ("sbuf", [128, 272], "bfloat16")
-for _c in range(2):
-    SCRATCH["N0t%d" % _c] = ("sbuf", [128, 16], "uint16")
-    SCRATCH["N0q%d" % _c] = ("sbuf", [128, 16], "bfloat16")
-    SCRATCH["X1%d" % _c] = ("sbuf", [128, 256], "bfloat16")
-    SCRATCH["OA%d" % _c] = ("sbuf", [128, 256], "uint16")
-    SCRATCH["IA%d" % _c] = ("sbuf", [128, 256], "int32")
+SCRATCH = {}
+for _n, _w, _d in (
+        ("ip", 1, I32), ("ic", 8, I32), ("CF", 24, F32), ("RI", 512, I32), ("TBi", 32, I32), ("TB", 32, U16), ("NI", 32, I32),
+        ("ZF", 32, I32), ("ZG", 32, F32), ("ZH", 32, F32), ("CI", 16, F32),
+        ("jm1", 128, BF), ("gw", 192, BF), ("g4", 128, BF), ("c64", 128, BF), ("g32", 256, BF), ("WM", 128, BF), ("KC", 128, BF),
+        ("ones", 512, BF), ("Bw", 192, BF), ("TRI", 192, BF), ("HN", 192, BF), ("IB", 192, BF), ("NB", 192, BF),
+        ("P22", 128, BF), ("I", 128, BF), ("B2x", 128, BF), ("SW", 256, F32), ("SN", 512, BF), ("NT", 256, BF),
+        ("LG", 15 * 128, BF), ("LH", 16 * 128, BF), ("BH", 128, BF),
+        ("BX", 256, BF), ("MK", 256, BF), ("BD", 128, F32), ("EX", 16, U16), ("ZX", 256, F32), ("RS", 128, F32), ("YH", 8, F32),
+        ("XT", 128, F32), ("AM", 16, I32), ("ODD", 4 * NC + 2 * NV, F32), ("IO", 4 * NC + 4 * NV, I32),
+        ("CD", 64 * NC, BF), ("K0S", 128, F32), ("km", 128, F32), ("Y", 128, F32),
+        ("FS", 80, I32), ("K31", 16, I32), ("U", 32, I32), ("E1", 32, F32), ("E2", 32, F32), ("AI", 16, I32),
+        ("SEL", 16, U16), ("CODE", 16, U16), ("N1t", 16, U16), ("BS", 256, BF), ("OH", 256, BF), ("MD", 256, BF),
+        ("AR", 256, BF), ("PN", 256, BF), ("L0", 256, BF), ("L1", 256, BF)):
+    SCRATCH[_n] = ("sbuf", [128, _w], _d)
+for _s in range(2):
+    for _n, _w, _d in (("S", 4096, BF), ("X", 128, BF), ("XE", 16 * NV, BF), ("OV", 4 * NV, U16), ("OC", 4 * NC, U16),
+                       ("DZ", 160, BF), ("DO", 160, I32), ("N0t", 16, U16), ("FT", 16, F32), ("TO", 96, F32),
+                       ("CM", 4 * NC + 2 * NV, BF), ("ZB", 128, BF),
+                       ("OUT", 256, F32), ("ZI", 16, F32), ("ZT", 256, F32)):
+        SCRATCH[_n + str(_s)] = ("sbuf", [128, _w], _d)
+    for _t in range(4):
+        SCRATCH["W%d%d" % (_s, _t)] = ("sbuf", [128, 768], BF)
     for _v in range(2):
-        SCRATCH["DA%d%d" % (_c, _v)] = ("sbuf", [128, 2048], "bfloat16")
-        SCRATCH["DB%d%d" % (_c, _v)] = ("sbuf", [128, 16 * NB], "bfloat16")
-    for _n in ("K0S", "km", "XT"):
-        SCRATCH[_n + str(_c)] = ("sbuf", [128, 128], "float32")
-for _n in ("OUT", "ZO", "ZR"):
-    SCRATCH[_n] = ("sbuf", [128, 256], "float32")
-SCRATCH["Y"] = ("sbuf", [128, 256], "int32")
-for _n in ("CR", "CT", "OH", "BS", "MD"):
-    SCRATCH[_n] = ("sbuf", [128, 256], "bfloat16")
-SCRATCH["ZC"] = ("sbuf", [128, 256], "int32")
+        SCRATCH["D%d%d" % (_s, _v)] = ("sbuf", [128, 16 * NV], BF)
+        SCRATCH["R%d%d" % (_s, _v)] = ("sbuf", [128, 16 * NV], BF)
+SCRATCH["ST"] = ("sbuf", [128, 8, 32], BF)
+PSUM = ("K0", "K1", "PO0", "PO1", "AL", "DD", "SM", "N1")
+for _n in PSUM:
+    SCRATCH[_n] = ("psum", [128, 512], F32)
 
-NDMA = 16
-SEMAPHORES = ["sV", "sA", "sP", "sG", "sL"] + ["d%d" % k for k in range(NDMA)] + ["arr%d" % k for k in range(4)]
-PSUM = ("KA0", "KA1", "KB0", "KB1", "PO0", "PO1", "MI1", "MI2")
+NDMA = 40
+SEMAPHORES = (["sV", "sA", "sP", "sG", "sL", "dF"] + ["d%d" % k for k in range(NDMA)]
+              + ["arr%d%d" % (s, t) for s in range(2) for t in range(4)])
 
 
 def rank_program(g, core, T, topo):
@@ -71,7 +51,7 @@ def rank_program(g, core, T, topo):
     NR_ = len(T.cores)
     queues = {"V": g.vector, "A": g.scalar, "P": g.tensor, "G": g, "S": g.sync}
 
-    ops, last, ndma, sent, compn = [], {}, [0], [0], {}
+    ops, last, ndma, sent, compn, begun = [], {}, [0], [0], {}, []
 
     def norm(x):
         if isinstance(x, str):
@@ -107,11 +87,12 @@ def rank_program(g, core, T, topo):
         deps.discard(me)
         ops.append({"q": q, "fn": fn, "deps": deps, "comp": comp, "ci": ci, "amt": amt, "sig": amt != 1, "need": []})
 
-    def dma(q, out, in_, r=(), w=()):
-        k = ndma[0]
-        ndma[0] += 1
+    def dma(q, out, in_, r=(), w=(), comp=None):
+        if comp is None:
+            comp = "d%d" % ndma[0]
+            ndma[0] += 1
         qq = queues[q]
-        op(q, lambda: qq.dma_start(out, in_), r, w, "d%d" % k, 16)
+        op(q, lambda: qq.dma_start(out, in_), r, w, comp, 16)
 
     def V(name, r, w, *a, **k):
         fn = {"tt": g.vector.tensor_tensor, "ts": g.vector.tensor_scalar, "cp": g.vector.tensor_copy, "tr": g.vector.transpose,
@@ -121,8 +102,8 @@ def rank_program(g, core, T, topo):
     def A(r, w, out, in_, func, **k):
         op("A", lambda: g.scalar.activation(out, in_, func, **k), r, w)
 
-    def mm(r, w, out, lhsT, rhs, start, stop):
-        op("P", lambda: g.tensor.matmul(out, lhsT, rhs, start, stop), r, w)
+    def mm(r, bank, out, lhsT, rhs, start=False, stop=False):
+        op("P", lambda: g.tensor.matmul(out, lhsT, rhs, start, stop), r, [bank])
 
     def iota(w, out, pattern, base, cm, small=True):
         if small:
@@ -130,376 +111,474 @@ def rank_program(g, core, T, topo):
         else:
             op("G", lambda: g.iota(out, pattern, base, cm), (), w)
 
-    def swap(bank, ap, r):
-        for y in range(2):
-            for x in range(2):
-                mm(["SW"] + r, [bank], T[bank][:, y:16:2], T.SW[:, 128 * (2 * y + x):128 * (2 * y + x) + 128], ap(x), x == 0, x == 1)
-
-    def send(t, dst):
+    def send(s, t):
+        dst = T.cores[(rank - 1 - t % (NR_ - 1)) % NR_]
         rid, pid, _ = topo.addr(dst)
         m = topo.mask(core, dst)
         sent[0] += len(topo.engines(core, dst))
-        out, src = T["W%d" % t][:, 256:528], T["ST%d" % t][:]
-        op("G", lambda: g.remote_dma(out, src, T.sem["arr%d" % t], T.sem.sL, pid, rid, m), ["ST%d" % t], (), "sL", 0)
+        w = "W%d%d" % (s, t)
+        op("G", lambda: g.remote_dma(T[w][:, 256:512], T[w][:, 0:256], T.sem["arr%d%d" % (s, t)], T.sem.sL, pid, rid, m),
+           [(w, 0, 256)], (), "sL", 0)
 
-    def recv(t, src):
-        op("N", None, (), [("W%d" % t, 256, 528)], "arr%d" % t, len(topo.engines(src, core)))
+    def recv(s, t):
+        src = T.cores[(rank + 1 + t % (NR_ - 1)) % NR_]
+        op("N", None, (), [("W%d%d" % (s, t), 256, 512)], "arr%d%d" % (s, t), len(topo.engines(src, core)))
 
-    dma("S", T.RI[:], T.resid[:], (), ["RI"])
-    dma("A", T.SI[:], T.src0[:], (), ["SI"])
-    dma("S", T.NI[:], T.nx0[:], (), ["NI"])
-    dma("A", T.X[:], T.obs[:], (), ["X"])
-    dma("S", T.S[:, 0:2048], T.prof[:, 0:2048], (), [("S", 0, 2048)])
-    dma("A", T.S[:, 2048:4096], T.prof[:, 2048:4096], (), [("S", 2048, 4096)])
+    def half(h):
+        return slice(64 * h, 64 * h + 64)
 
-    iota(["ip"], T.ip[:], [[0, 1]], 0, 1, False)
-    iota(["dm"], T.dm[:], [[1, 128]], 0, -1)
-    V("set", (), ["FI"], T.FI[:], 0)
-    dma("S", T.FI[0:128:16, :], T.fit0[:], (), ["FI"])
-    iota(["gm"], T.gm[:], [[1, 8], [0, 16]], 0, 0)
-    iota(["jm1"], T.jm1[:], [[0, 8], [1, 16]], 1, 0)
-    iota(["jb"], T.jb[:], [[0, 8], [1, 16]], -20, 0)
-    iota(["jw"], T.jw[:], [[0, 16], [1, 16]], 0, 0)
-    V("ts", ["ip"], [("ic", 0, 1)], T.ic[:, 0:1], T.ip[:], 15, None, OP.bitwise_and)
-    V("ts", ["ip"], [("ic", 1, 2)], T.ic[:, 1:2], T.ip[:], 4, None, OP.arith_shift_right)
-    V("ts", ["ip"], [("ic", 2, 3)], T.ic[:, 2:3], T.ip[:], 4, 1, OP.arith_shift_right, OP.bitwise_and)
-    V("ts", ["ip"], [("ic", 3, 4)], T.ic[:, 3:4], T.ip[:], 31, None, OP.bitwise_and)
-    V("ts", ["ip"], [("ic", 4, 5)], T.ic[:, 4:5], T.ip[:], 5, None, OP.arith_shift_right)
-
-    def col(k, s, m, a):
-        V("ts", [("ic", s, s + 1)], [("CF", k, k + 1)], T.CF[:, k:k + 1], T.ic[:, s:s + 1], float(m), float(a), OP.mult, OP.add)
+    for s in range(2):
+        dma("SA"[s], T.RI[0:64, 256 * s:256 * s + 256], T.resid[half(s), :], (), [("RI", s, s + 1)])
+        dma("AS"[s], T.TBi[64:128, 16 * s:16 * s + 16], T.src0[half(s), :], (), [("TBi", s, s + 1)])
+    for s in range(2):
+        for h in range(2):
+            dma("SA"[h], T.NI[half(h), 16 * s:16 * s + 16], T.nx0[half(s), :], (), [("NI", 2 * s + h, 2 * s + h + 1)])
+            dma("SA"[h], T["X%d" % s][half(h), :], T.obs[half(s), 128 * h:128 * h + 128], (), [("X%d" % s, h, h + 1)])
+    for h in range(2):
+        dma("SA"[h], T.S0[half(h), :], T.prof[half(0), :], (), [("S0", h, h + 1)])
+    for k in range(16):
+        h, al, s, e = k >> 3, (k >> 2) & 1, (k >> 1) & 1, k & 1
+        p0, gr = 64 * h + 32 * al + 16 * s, 4 * s + 2 * al + e
+        dma("S", T.ZF[p0:p0 + 16, 16 * e:16 * e + 16], T.fit0[gr:gr + 1, :], (), [("ZF", k, k + 1)], "dF")
 
     def C(k):
         return T.CF[:, k:k + 1]
-    col(3, 2, 1, 0)
-    col(4, 2, -1, 1)
-    col(0, 0, 1, 1)
-    col(1, 0, 1, -20)
-    col(2, 1, 1, 0)
-    col(5, 0, 1, 0)
-    col(6, 3, 1, 0)
-    col(7, 4, 1, 0)
-    for y in range(2):
-        for x in range(2):
-            s = 128 * (2 * y + x)
-            V("ts", ["dm", ("CF", 3, 5)], [("SW", s, s + 128)], T.SW[:, s:s + 128], T.dm[:], float(16 * (x - y)), C(3 if y else 4),
-              OP.is_equal, OP.mult)
-    V("cp", ["SI"], [("SN", 0, 16)], T.SN[:, 0:16], T.SI[:])
-    V("cp", ["NI"], [("SN", 16, 32)], T.SN[:, 16:32], T.NI[:])
-    V("cp", ["NI"], ["N0t0"], T.N0t0[:], T.NI[:])
-    V("cp", ["RI"], [("ST0", 0, 256)], T.ST0[:, 0:256], T.RI[:])
-    swap("MI1", lambda x: T.SN[:, x:16:2], [("SN", 0, 16)])
-    V("cp", ["MI1"], [("ST0", 256, 272)], T.ST0[:, 256:272], T.MI1[:, 0:16])
-    send(0, T.cores[(rank - 1) % NR_])
-    swap("MI2", lambda x: T.SN[:, 16 + x:32:2], [("SN", 16, 32)])
-    V("cp", ["MI2"], ["N0q0"], T.N0q0[:], T.MI2[:, 0:16])
-    iota(["ODD0"], T.ODD0[:], [[0, 2], [2, 128]], 1, 0)
-    NX = 128 + NB
-    for k in range(16):
-        A(["X"], [("XEk", k, k + 1)], T.XE[:, k:16 * NX:16], T.X[:, 0:NX], AF.Copy)
-    V("set", (), ["ones"], T.ones[:], 1.0)
-    V("set", (), [("JK", 256, 384)], T.JK[0:1, 256:384], 4096.0)
-    V("set", (), ["J16"], T.J16[0:1, :], 16.0)
-    V("cp", ["jw"], ["EX"], T.EX[:], T.jw[:, 0:16])
-    V("ts", ["jw"], ["KM"], T.KM[:], T.jw[:], 0.0, None, OP.is_gt)
-    V("ts", ["gm", "CF"], ["B"], T.B[:], T.gm[:], C(2), None, OP.is_equal)
-    V("ts", ["B"], ["BX"], T.BX[:], T.B[:], 32.0, None, OP.mult)
-    V("tt", ["jm1", "B"], ["JA"], T.JA[:], T.jm1[:], T.B[:], OP.mult)
-    V("tt", ["jb", "B"], ["JB"], T.JB[:], T.jb[:], T.B[:], OP.mult)
-    V("ts", ["JA", "CF"], ["TRI"], T.TRI[:], T.JA[:], C(0), None, OP.is_ge)
-    V("ts", ["JB", "CF"], ["HN"], T.HN[:], T.JB[:], C(1), -1.0, OP.is_lt, OP.mult)
-    V("ts", ["JA", "CF"], ["I"], T.I[:], T.JA[:], C(0), None, OP.is_equal)
-    V("tt", ["I", "B"], ["IB"], T.IB[:], T.I[:], T.B[:], OP.subtract)
-    V("ts", ["B"], ["NBM"], T.NBM[:], T.B[:], -1.0, None, OP.mult)
-    V("ts", ["I"], ["P22"], T.P22[:], T.I[:], float(2 ** 22), None, OP.mult)
-    V("ts", ["jw"], ["RS"], T.RS[:], T.jw[:, 0:128], 0.0, BIG, OP.is_equal, OP.mult)
-    for k in range(4):
-        V("ts", ["JA"], [("LG", k, k + 1)], T.LG[:, 128 * k:128 * k + 128], T.JA[:], float(k + 1), 32.0, OP.is_gt, OP.mult)
 
-    def step(name, k, base, m):
-        out = T[name][:, 128 * k:128 * k + 128]
-        op("G", lambda: g.affine_select(out, T.BX[:], [[0, 8], [m, 16]], OP.is_ge, 0.0, base, 0), ["BX"], [(name, k, k + 1)])
-    for k in range(4, 15):
-        step("LG", k, -k - 1, 1)
-    iota(["ODDC"], T.ODDC[:], [[2, NC], [0, 4]], 257 + 2 * NB, 0)
-    iota([("JK", 0, 256)], T.JK[0:1, 0:256], [[16, 2], [0, 8], [1, 16]], 0, 0)
+    def bits(k, sh, m):
+        V("ts", ["ip"], [("ic", k, k + 1)], T.ic[:, k:k + 1], T.ip[:], sh, m, OP.arith_shift_right, OP.bitwise_and)
+
+    def col(k, s, m, a):
+        V("ts", [("ic", s, s + 1)], [("CF", k, k + 1)], C(k), T.ic[:, s:s + 1], float(m), float(a), OP.mult, OP.add)
+
+    def numbers(s, t):
+        w = "W%d%d" % (s, t)
+        iota([(w, 512, 768)], T[w][:, 512:768], [[1, 256]], 0, 0)
+    iota(["ip"], T.ip[:], [[0, 1]], 0, 1, False)
+    iota(["CI"], T.CI[:], [[16, 16]], 0, 0)
+    numbers(0, 0)
+    iota(["gw"], T.gw[:], [[1, 12], [0, 16]], -4, 0)
+    iota(["c64"], T.c64[:], [[0, 2], [1, 64]], 0, 0)
+    iota(["g32"], T.g32[:], [[1, 8], [0, 32]], 0, 0)
+    for k, (sh, m) in enumerate(((0, 15), (4, 3), (6, 1), (5, 3), (4, 1), (3, 6))):
+        bits(k, sh, m)
+    col(7, 0, 1, 0)
+    col(0, 0, 1, 1)
+    V("ts", ["CI", ("CF", 7, 8)], ["CI"], T.CI[:], T.CI[:], C(7), None, OP.add)
+    col(3, 1, 1, 0)
+    for s in range(2):
+        V("cp", ["CI"], [("TBi", 2 + s, 3 + s)], T.TBi[0:64, 16 * s:16 * s + 16], T.CI[0:64, :])
+    col(5, 4, -1, 1)
+    col(6, 4, 1, 0)
+    col(8, 2, 256, 256)
+    col(9, 2, 256, 1)
+    V("tt", [("ic", 2, 3), ("ic", 5, 6)], [("CF", 2, 3)], C(2), T.ic[:, 5:6], T.ic[:, 2:3], OP.add)
+    for s in range(2):
+        V("cp", [("W00", 512, 768)], [("RI", 2 + s, 3 + s)], T.RI[64:128, 256 * s:256 * s + 256], T.W00[64:128, 512:768])
+    for s in range(2):
+        V("cp", [("TBi", s, s + 1), ("TBi", 2 + s, 3 + s)], [("TB", s, s + 1)], T.TB[:, 16 * s:16 * s + 16], T.TBi[:, 16 * s:16 * s + 16])
+        w = "W%d0" % s
+        V("cp", [("RI", s, s + 1), ("RI", 2 + s, 3 + s), ("TB", s, s + 1)], [(w, 0, 256)], T[w][:, 0:256],
+          T.RI[:, 256 * s:256 * s + 256].indirect(T.TB[:, 16 * s:16 * s + 16]))
+        send(s, 0)
+    V("ts", ["gw", ("CF", 3, 4)], ["Bw"], T.Bw[:], T.gw[:], C(3), None, OP.is_equal)
+    V("ts", ["gw", ("CF", 3, 4)], ["NB"], T.NB[:], T.gw[:], C(3), -1.0, OP.is_equal, OP.mult)
+    V("ts", ["g32", ("CF", 2, 3)], ["BX"], T.BX[:], T.g32[:], C(2), 32.0, OP.is_equal, OP.mult)
+    V("ts", ["gw", ("CF", 2, 3)], ["BH"], T.BH[:], T.gw[:, 64:192], C(2), 32.0, OP.is_equal, OP.mult)
+    V("set", (), ["ones"], T.ones[:], 1.0)
+    V("set", (), ["KC"], T.KC[0:1, :], 4096.0)
+    bits(6, 4, 7)
+    bits(7, 0, 32)
+    V("ts", [("CF", 7, 8)], [("CF", 1, 2)], C(1), C(7), 0.0, 256.0, OP.is_equal, OP.mult)
+    col(14, 6, 1, 0)
+    for k, src, r, m in ((4, T.ic[:, 3:4], ("ic", 3, 4), 16.0), (15, T.ic[:, 7:8], ("ic", 7, 8), 1.0), (16, C(2), ("CF", 2, 3), 16.0)):
+        V("ts", [r, ("CF", 7, 8)], [("CF", k, k + 1)], C(k), src, m, C(7), OP.mult, OP.add)
+    V("cp", ["ip"], [("CF", 17, 18)], C(17), T.ip[:])
+    for k, src in ((18, 4), (20, 15)):
+        for b in range(2):
+            V("ts", [("CF", 5, 7), ("CF", src, src + 1)], [("CF", k + b, k + b + 1)], C(k + b), C(6 - b), 1000.0, C(src), OP.mult, OP.add)
+    V("ts", [("CF", 7, 8), ("CF", 1, 2)], [("CF", 10, 11)], C(10), C(7), 1.0, C(1), OP.is_equal, OP.add)
+    for k, m, a in ((11, -255.0 / 65536, 1.0), (12, -127.5 / 65536, 0.0), (13, 1.0 / 16, 0.0)):
+        V("ts", [("CF", 1, 2)], [("CF", k, k + 1)], C(k), C(1), m, a, OP.mult, OP.add)
+
+    def keep(out, in_, pattern, cmp, base, cm):
+        op("G", lambda: g.affine_select(T[out][:], T[in_][:], pattern, cmp, 0.0, base, cm), [in_], [out])
+    keep("ST", "BX", [[0, 8], [1, 32]], OP.is_ge, -16, 0)
+    keep("TRI", "Bw", [[1, 192]], OP.is_ge, -64, -1)
+    keep("HN", "NB", [[-1, 192]], OP.is_gt, 64, 1)
+    keep("IB", "NB", [[1, 192]], OP.not_equal, -64, -1)
+    iota(["jm1"], T.jm1[:], [[0, 8], [1, 16]], 1, 0)
+    iota(["g4"], T.g4[:], [[0, 2], [1, 4], [0, 16]], 0, 0)
     for k in range(16):
-        step("LH", k, k, -1)
-    iota(["ODDB"], T.ODDB[:], [[0, 4], [2, NB]], 257, 0)
-    iota(["IQ"], T.IQ[:], [[32, 8], [0, 2]], -256, 0)
-    iota(["gm2"], T.gm2[:], [[1, 4], [0, 32]], 0, 0)
+        op("G", lambda k=k: g.affine_select(T.LH[:, 128 * k:128 * k + 128], T.BH[:], [[0, 8], [-1, 16]], OP.is_ge, 0.0, k, 0),
+           ["BH"], [("LH", k, k + 1)])
+    numbers(1, 0)
+    for s in range(2):
+        for k in range(16):
+            A(["X%d" % s], [("XE%d" % s, k, k + 1)], T["XE%d" % s][:, k:16 * NV:16], T["X%d" % s][:, 0:NV], AF.Copy)
+    J = T.jm1[:, 0:128]
+    for s in range(2):
+        V("cp", [("NI", 2 * s, 2 * s + 2)], ["N0t%d" % s], T["N0t%d" % s][:], T.NI[:, 16 * s:16 * s + 16])
+        V("cp", [("NI", 2 * s, 2 * s + 2)], [("DO%d" % s, 1, 2)], T["DO%d" % s][:, 1:80:5], T.NI[:, 16 * s:16 * s + 16])
+    V("ts", ["gw", "CF"], ["WM"], T.WM[:], T.gw[:, 64:192], C(14), C(10), OP.is_equal, OP.mult)
+    num, rnum = T.W00[:, 512:640], ("W00", 512, 768)
+    for k in range(6):
+        o, a, b = (T.ODD[:, k:4 * NC:4], NV, 128) if k < 4 else (T.ODD[:, 4 * NC + NV * (k - 4):4 * NC + NV * (k - 3)], 0, NV)
+        A([rnum, ("CF", 9, 10)], [("ODD", k, k + 1)], o, T.W00[:, 512 + a:512 + b], AF.Identity, bias=C(9), scale=2.0)
+
+    def keyconsts():
+        for b in range(2):
+            for e in range(2):
+                k = 2 * b + e
+                V("ts", ["c64", "CF"], [("SN", k, k + 1)], T.SN[:, 128 * k:128 * k + 128], T.c64[:], C(20 + b), 16.0 * e,
+                  OP.subtract, OP.is_equal)
+        V("ts", [rnum, "CF"], ["P22"], T.P22[:], num, C(16), float(2 ** 22), OP.is_equal, OP.mult)
+        V("ts", [rnum, "CF"], ["I"], T.I[:], num, C(17), None, OP.is_equal)
+        V("set", (), ["SM"], T.SM[:, 48:64], 0.0)
+        V("ts", ["gw", "CF"], ["BD"], T.BD[:], T.gw[:, 64:192], C(14), None, OP.is_equal)
+        V("cp", [rnum], ["EX"], T.EX[:], T.W00[:, 512:528])
+        for b in range(2):
+            V("ts", ["c64", "CF"], [("SW", b, b + 1)], T.SW[:, 128 * b:128 * b + 128], T.c64[:], C(18 + b), None, OP.is_equal)
+        for s in range(2):
+            dz, do = "DZ%d" % s, "DO%d" % s
+            for k, c in ((0, 0.0), (2, 1.0), (4, 416.0)):
+                A(["ones"], [(dz, k, k + 1)], T[dz][:, k:80:5], T.ones[:, 0:16], AF.Copy, scale=c)
+            V("ts", ["CI", "CF"], [(do, 2, 3)], T[do][:, 2:80:5], T.CI[:], -1.0, C(8), OP.mult, OP.add)
+            V("cp", ["CI"], [(do, 3, 4)], T[do][:, 3:80:5], T.CI[:])
+        for k in range(15):
+            V("cp", ["ST"], [("LG", k, k + 1)], T.LG[:, 128 * k:128 * k + 128], T.ST[:, :, 15 - k:31 - k])
 
     def lastconsts():
-        V("cp", ["FI"], [("FF", 0, 256)], T.FF[:, 0:256], T.FI[:])
-        V("tr", [("FF", 0, 256)], [("FF", 256, 512)], T.FF[:, 256:512], T.FF[:, 0:256])
-        V("cp", [("FF", 256, 512)], ["F"], T.F[:], T.FF[:, 256:512:16])
-        V("ts", ["F"], ["FT"], T.FT[:], T.F[:], 32.0, None, OP.mult)
-        V("ts", ["IQ", "CF"], ["IQ"], T.IQ[:], T.IQ[:], C(6), None, OP.add)
-        V("ts", ["gm2", "CF"], ["B32"], T.B32[:], T.gm2[:], C(7), None, OP.is_equal)
-        V("set", (), ["AS"], T.AS[:], 0.0)
-        V("set", (), ["ZC"], T.ZC[:], 0)
-        V("set", (), ["D0"], T.D0[:], 0)
-        for k in (1, 3):
-            V("ts", ["IQ"], [("D0", k, k + 1)], T.D0[:, k:80:5], T.IQ[:], 0.0, 1.0, OP.mult, OP.add)
-        V("ts", ["IQ"], [("D1", 3, 4)], T.D1[:, 3:80:5], T.IQ[:], -1.0, None, OP.mult)
-        V("cp", ["IQ"], [("D1", 4, 5)], T.D1[:, 4:80:5], T.IQ[:])
-        V("set", (), ["ZO"], T.ZO[:], 0.0)
+        V("ts", ["jm1"], ["RS"], T.RS[:], J, 1.0, BIG, OP.is_equal, OP.mult)
+        V("ts", ["g4", "CF"], ["B2x"], T.B2x[:], T.g4[:], C(3), 32.0, OP.is_equal, OP.mult)
+        for k in range(2):
+            V("ts", ["jm1", "CF"], [("MK", k, k + 1)], T.MK[:, 128 * k:128 * k + 128], J, C(0), None, OP.is_equal)
+        V("ts", ["RS"], ["RS"], T.RS[:], T.RS[:], -1.0, None, OP.add)
 
-    for t in range(4):
-        par = t & 1
-        W, Wn = T["W%d" % t], "W%d" % t
-        ST, STn = T["ST%d" % t], "ST%d" % t
-        n0t, n0q, x1 = "N0t%d" % par, "N0q%d" % par, "X1%d" % par
-        m0, mt = "N0q%d" % (1 - par), "N0t%d" % (1 - par)
-        n1q = T[x1][:, 0:256:16]
-        recv(t, T.cores[(rank + 1 + t % (NR_ - 1)) % NR_])
+    def fit(step):
+        if step == 0:
+            V("ts", ["ZF"], ["ZG"], T.ZG[:], T.ZF[:], 32.0, None, OP.mult)
+        if step == 1:
+            V("tr", ["ZG"], ["ZH"], T.ZH[:], T.ZG[:])
+        for s in range(2 if step == 2 else 0):
+            do = "DO%d" % s
+            V("cp", ["ZH"], [(do, 5, 6)], T[do][:, 81:160:5], T.ZH[:, 16 * s:16 * s + 16])
+            V("cp", ["ZH"], ["FT%d" % s], T["FT%d" % s][:], T.ZH[:, 16 * s:16 * s + 16])
 
-        def pos0(v, bank, a, b, o):
-            mm([("JK", 256, 384), "ones"], [bank], o, T.JK[0:1, 256:384], T.ones[0:1, 0:b - a], True, False)
-            if v:
-                mm(["B", ("ST0", 0, 256)], [bank], o, T.B[:], T.ST0[:, a:b], False, False)
+    def wide(name, h):
+        return T[name][0:64, 64 - 64 * h:192 - 64 * h]
 
-        def pos1(c, v, bank, a, b, o):
-            m = "HN" if v else "TRI"
-            mm([m, ("L%d" % c, a, b)], [bank], o, T[m][:], T["L%d" % c][:, a:b], False, True)
+    def places(c, v):
+        o = T.PO1[:, 4 * NC + NV * v:4 * NC + NV * v + NV] if c else T.PO0[:, NV * v:NV * v + NV]
+        return (("PO%d" % c, o, 0, NV), ("PO1", T.PO1[:, 2 * c + v:4 * NC:4], NV, 128))
 
-        def pos(c, v, bank, a, b, o):
-            pos0(v, bank, a, b, o)
-            pos1(c, v, bank, a, b, o)
+    def pos0(s):
+        cm, zb = "CM%d" % s, "ZB%d" % s
+        mm(["WM", cm], "PO0", T.PO0[:, 0:2 * NV], T.WM[:], T[cm][:, 4 * NC:4 * NC + 2 * NV], True)
+        mm(["WM", cm], "PO1", T.PO1[:, 0:4 * NC + 2 * NV], T.WM[:], T[cm][:], True)
+        for c in range(2):
+            mm(["WM", zb], "AL", T.AL[:, c:256:2], T.WM[:], T[zb][:], c == 0)
 
-        def allowed(c):
-            mm(["B", ("ST0", 0, 256)], ["MI1"], T.MI1[:, 0:256], T.B[:], T.ST0[:, 0:256], True, False)
-            mm(["IB", "L%d" % c], ["MI1"], T.MI1[:, 0:256], T.IB[:], T["L%d" % c][:, 0:256], False, True)
-            A(["MI1"], [("AR", c, c + 1)], T.AR[:, 256 * c:256 * c + 256], T.MI1[:, 0:256], AF.Abs, bias=-127.5)
+    def mass(s):
+        w, cm, zb, bank = "W%d0" % s, "CM%d" % s, "ZB%d" % s, ("DD", "SM")[s]
+        ib, ri = T.IO[:, 128 * s:128 * s + 128], ("IO", 128 * s, 128 * s + 128)
+        mm(["KC", "ones"], bank, T[bank][:, 0:128], T.KC[0:1, :], T.ones[0:1, 0:128], True)
+        for h in range(2):
+            mm(["Bw", (w, 0, 256)], bank, T[bank][:, 0:128], wide("Bw", h), T[w][0:64, 128 * h:128 * h + 128], False, h == 1)
+        A(["ones", "CF"], [cm], T[cm][:], T.ones[:, 0:4 * NC + 2 * NV], AF.Copy, scale=C(13))
 
-        def offsets(bank, odd, o, a, b):
-            In = "IBo" if o == "OB" else "I" + o[1:]
-            ib = T[In][:, a:b]
-            V("tt", [bank, odd], [(In, a, b)], ib, T[bank][:, 0:b - a], T[odd][:, 0:b - a], OP.mult)
-            V("ts", [(In, a, b)], [(In, a, b)], ib, ib, 2, 4095, OP.arith_shift_right, OP.bitwise_and)
-            V("cp", [(In, a, b)], [(o, a, b)], T[o][:, a:b], ib)
-
-        def gat(c, v, s, n0=0, n1=None):
-            d = "D%s%d%d" % (s, c, v)
-            o, k = ("OA%d" % c, 128 * v) if s == "A" else ("OB", NB * (2 * c + v))
-            n1 = (128 if s == "A" else NB) if n1 is None else n1
-            xb = 0 if s == "A" else 2048
-            V("tt", ["S", "XEk", (o, k + n0, k + n1)], [(d, 16 * n0, 16 * n1)], T[d][:, 16 * n0:16 * n1],
-              T.S[:, 0:4096].indirect(T[o][:, k + n0:k + n1]), T.XE[:, xb + 16 * n0:xb + 16 * n1], OP.subtract)
-
-        def absv(c, v, s, n0=0, n1=None):
-            d = "D%s%d%d" % (s, c, v)
-            n1 = (128 if s == "A" else NB) if n1 is None else n1
-            A([(d, 16 * n0, 16 * n1)], [(d, 16 * n0, 16 * n1)], T[d][:, 16 * n0:16 * n1], T[d][:, 16 * n0:16 * n1], AF.Abs)
-
-        def keystart(c, bank, a, b, sl):
-            mm([("JK", 0, 256), "ones"], [bank], T[bank][:, a:b], T.JK[0:1, 128 * c:128 * c + 128], T.ones[0:1, 0:b - a], True, False)
-            mm(["P22", "PN"], [bank], T[bank][:, a:b], T.P22[:], T.PN[:, 256 * c + sl:256 * c + sl + b - a], False, False)
-
-        def keys(c, v, s, bank):
-            d = "D%s%d%d" % (s, c, v)
-            n = 128 if s == "A" else NB
-            if v == 0:
-                keystart(c, bank, 0, n, 0 if s == "A" else 128)
-            for k in range(15 + v):
-                l = "LH" if v else "LG"
-                mm([(l, k, k + 1), d], [bank], T[bank][:, 0:n], T[l][:, 128 * k:128 * k + 128], T[d][:, k:16 * n:16], False, v == 1 and k == 15)
-
-        def cslots(a, b):
-            for s in range(a, b):
-                i = 256 - NC + s
-                A(["S", "OC", "X"], [("CD", s, s + 1)], T.CD[:, 64 * s:64 * s + 64], T.S[:, 0:4096].indirect(T.OC[:, 4 * s:4 * s + 4]), AF.Abs,
-                  bias=T.X[:, i:i + 1], scale=-1.0)
-
-        def keysc(s0, s1):
-            n, o = s1 - s0, T.KB0[:, 256 + 2 * s0:256 + 2 * s1]
-            mm([("JK", 0, 256), "ones"], ["KB0"], o, T.JK[0:1, 0:128], T.ones[0:1, 0:2 * n], True, False)
-            mm(["J16", "ones"], ["KB0"], T.KB0[:, 257 + 2 * s0:256 + 2 * s1:2], T.J16[0:1, :], T.ones[0:1, 0:n], False, False)
+        def spread():
+            V("cp", [ri], [zb], T[zb][:], ib)
+            A([zb], [cm], T[cm][:, 4 * NC + NV:], T[zb][:, 0:NV], AF.Copy)
             for c in range(2):
-                i = 256 * c + 256 - NC
-                mm(["P22", "PN"], ["KB0"], T.KB0[:, 256 + 2 * s0 + c:256 + 2 * s1:2], T.P22[:], T.PN[:, i + s0:i + s1], False, False)
-            for v in range(2):
-                l = "LH" if v else "LG"
-                for k in range(15 + v):
-                    mm([(l, k, k + 1), ("CD", s0, s1)], ["KB0"], o, T[l][:, 128 * k:128 * k + 128],
-                       T.CD[:, 64 * s0 + 16 * v + k:64 * s1:32], False, v == 1 and k == 15)
+                A([zb], [cm], T[cm][:, 2 * c + 1:4 * NC:4], T[zb][:, NV:128], AF.Copy)
+        return [lambda: V("ts", [bank, "CF"], [ri], ib, T[bank][:, 0:128], C(11), C(12), OP.mult, OP.add),
+                lambda: V("ts", [ri], [ri], ib, ib, 255, None, OP.bitwise_and), spread]
 
-        def I_(k):
-            return T.TI[:, 16 * k:16 * k + 16]
-
-        def F_(k):
-            return T.TF[:, 16 * k:16 * k + 16]
-
-        def ri(k):
-            return ("TI", k, k + 1)
-
-        def rf(k):
-            return ("TF", k, k + 1)
-        key, acc, nsel = T.Y[:, 15:256:16], T.D0[:, 4:80:5], T.FS[:, 2:80:5]
-
-        def n0steps(n, r):
-            V("ts", r, [("D1", 1, 2)], T.D1[:, 1:80:5], n, -1.0, None, OP.mult)
-            V("cp", r, [("D1", 2, 3)], T.D1[:, 2:80:5], n)
-
-        def best(h):
-            x, a, b = str(h), 128 * h, 128 * h + 128
-            k1 = "KA1" if h == 0 else "KB1"
-            n = 128 if h == 0 else NB
-            V("tt", [k1, ("K0S" + x, 0, n)], [("km" + x, 0, n)], T["km" + x][:, 0:n], T[k1][:, 0:n], T["K0S" + x][:, 0:n], OP.min)
-            V("tr", ["km" + x], ["XT" + x], T["XT" + x][:], T["km" + x][:])
-            V("scan", ["RS", "XT" + x], [("Y", a, b)], T.Y[:, a:b], T.RS[:], T["XT" + x][:], BIG, OP.add, OP.min)
-
-        def site(h, part):
-            a, b = 128 * h, 128 * h + 128
-            if part == 0:
-                V("ts", [("Y", a, b)], [("ZC", a, b)], T.ZC[:, a:b:16], T.Y[:, a + 15:b:16], 15, None, OP.bitwise_and)
-                V("scan", ["KM", ("ZC", a, b)], [("CR", a, b)], T.CR[:, a:b], T.KM[:, a:b], T.ZC[:, a:b], 0.0, OP.mult, OP.add)
-                V("tr", [("CR", a, b)], [("CT", a, b)], T.CT[:, a:b], T.CR[:, a:b])
-            else:
-                V("ts", [("CT", a, b), "CF"], [("OH", a, b)], T.OH[:, a:b], T.CT[:, a:b], C(5), None, OP.is_equal)
-
-        def accept():
-            V("ts", ["Y"], [("D0", 2, 3)], T.D0[:, 2:80:5], key, 4, 1, OP.arith_shift_right, OP.bitwise_and)
-            V("tt", ["Y", "FT"], [("D0", 4, 5)], acc, key, T.FT[:], OP.is_lt)
-            V("scan", ["D0", "D1"], ["FS"], T.FS[:], T.D0[:], T.D1[:], 0.0, OP.mult, OP.add)
-            swap("MI2", lambda x: T.FS[:, 4 + 5 * x:80:10], ["FS"])
-            site(1, 0)
-            V("ts", ["MI2"], ["SEL"], T.SEL[:], T.MI2[:, 0:16], 256.0, None, OP.add)
-            mm(["B", ("ST0", 0, 256)], ["MI1"], T.MI1[:, 0:256], T.B[:], T.ST0[:, 0:256], True, False)
-            V("cp", [(Wn, 0, 512), "SEL"], ["BS"], T.BS[:], W[:, 0:512].indirect(T.SEL[:, 0:16]))
-            mm(["NBM", "BS"], ["MI1"], T.MI1[:, 0:256], T.NBM[:], T.BS[:], False, True)
-            mm(["I", "BS"], ["MI2"], T.MI2[:, 0:256], T.I[:], T.BS[:], True, True)
-            site(1, 1)
-
-        def newlists(out, w):
-            V("tt", ["MI1", "OH"], ["MD"], T.MD[:], T.MI1[:, 0:256], T.OH[:], OP.mult)
-            V("tt", ["MI2", "MD"], w, out, T.MI2[:, 0:256], T.MD[:], OP.add)
-
-        def newsrc():
-            sn = "ST%d" % (t + 1)
-            so, wo = ST[:, 256:272], (STn, 256, 272)
-            V("tt", ["FS", wo], [rf(0)], F_(0), nsel, so, OP.subtract)
-            V("tt", [rf(0), ("D0", 4, 5)], [rf(1)], F_(1), F_(0), acc, OP.mult)
-            V("tt", [rf(1), wo], [(sn, 256, 272)], T[sn][:, 256:272], F_(1), so, OP.add)
-
-        def newnx(out, w):
-            V("ts", ["FS"], [rf(2)], F_(2), nsel, 416.0, None, OP.mult)
-            V("tt", [rf(2), "Y"], [ri(0)], I_(0), F_(2), key, OP.add)
-            V("ts", [ri(0)], [ri(1)], I_(1), I_(0), 5, 255, OP.arith_shift_right, OP.bitwise_and)
-            V("tt", [ri(1), x1], [rf(3)], F_(3), I_(1), n1q, OP.subtract)
-            V("tt", [rf(3), ("D0", 4, 5)], [rf(4)], F_(4), F_(3), acc, OP.mult)
-            V("tt", [rf(4), x1], w, out, F_(4), n1q, OP.add)
-
-        def newf(out, w):
-            V("ts", ["Y"], [ri(2)], I_(2), key, 5, None, OP.arith_shift_right)
-            V("tt", [ri(2), "F"], [rf(5)], F_(5), I_(2), T.F[:], OP.subtract)
-            V("tt", [rf(5), ("D0", 4, 5)], [rf(6)], F_(6), F_(5), acc, OP.mult)
-            V("tt", [rf(6), "F"], w, out, F_(6), T.F[:], OP.add)
-
-        PW = (Wn, 256, 512)
-        V("cp", [PW, n0t], [("L0", 0, 128)], T.L0[:, 0:128], W[:, 256:512].indirect(T[n0t][:, 0:8]))
-        A([(Wn, 512, 528), "EX"], ["XS"], T.XS[:], W[:, 512:528].indirect(T.EX[:, 0:16]), AF.Copy)
-        oA = T.PO0[:, 0:128]
-        pos0(0, "PO0", 0, 128, oA)
-        pos0(1, "PO1", 0, 128, T.PO1[:, 0:128])
-        pos1(0, 0, "PO0", 0, 128, oA)
-        pos1(0, 1, "PO1", 0, 128, T.PO1[:, 0:128])
-        V("tr", ["XS"], ["SR"], T.SR[:], T.XS[:])
-        A(["SR", n0t], ["NR"], T.NR[:], T.SR[:, 0:256].indirect(T[n0t][:, 0:16]), AF.Copy)
-        A([PW, n0t], [("L0", 128, 256)], T.L0[:, 128:256], W[:, 256:512].indirect(T[n0t][:, 8:16]), AF.Copy)
-        offsets("PO0", "ODD0", "OA0", 0, 128)
-        V("tr", ["NR"], [x1], T[x1][:], T.NR[:])
-        gat(0, 0, "A", 0, 64)
-        swap("MI2", lambda x: T[x1][:, 16 * x:256:32], [x1])
-        if t == 0:
-            A([(STn, 0, 256)], [(Wn, 0, 256)], W[:, 0:256], ST[:, 0:256], AF.Copy)
-        V("cp", ["MI2"], ["N1t"], T.N1t[:], T.MI2[:, 0:16])
-        offsets("PO1", "ODD0", "OA0", 128, 256)
-        A([PW, "N1t"], ["L1"], T.L1[:], W[:, 256:512].indirect(T.N1t[:, 0:16]), AF.Copy)
-        absv(0, 0, "A", 0, 64)
-        for c in range(2):
-            for v in range(2):
-                pos(c, v, "PO0", 256 - NC, 256, T.PO0[:, 2 * c + v:4 * NC:4])
-        allowed(0)
-        gat(0, 0, "A", 64, 128)
-        offsets("PO0", "ODDC", "OC", 0, 4 * NC)
-        allowed(1)
-        absv(0, 0, "A", 64, 128)
+    def pos1(c, part, stop):
+        L = "L%d" % c
         for v in range(2):
-            pos(1, v, "PO1", 0, 128, T.PO1[:, 128 * v:128 * v + 128])
+            bank, o, a, b = places(c, v)[part]
+            m = "HN" if v else "TRI"
+            for h in range(2):
+                mm([m, L], bank, o, wide(m, h), T[L][0:64, 128 * h + a:128 * h + b], False, stop and v == 1 and h == 1)
+
+    def allowed_mm():
         for c in range(2):
-            for v in range(2):
-                pos(c, v, "PO0", 128, 128 + NB, T.PO0[:, NB * (2 * c + v):NB * (2 * c + v) + NB])
-        V("ts", ["AR"], ["PN"], T.PN[:], T.AR[:], 127.5, None, OP.is_gt)
-        keys(0, 0, "A", "KA0")
-        cslots(0, CFIRST)
-        keysc(0, CFIRST)
-        gat(0, 1, "A")
-        absv(0, 1, "A")
-        keys(0, 1, "A", "KA0")
-        offsets("PO1", "ODD0", "OA1", 0, 256)
-        cslots(CFIRST, NC)
-        keysc(CFIRST, NC)
-        gat(1, 0, "A")
-        absv(1, 0, "A")
-        keys(1, 0, "A", "KA1")
-        A(["KA0"], ["K0S0"], T.K0S0[:], T.KA0[:, 0:128], AF.Copy)
-        gat(1, 1, "A")
-        offsets("PO0", "ODDB", "OB", 0, 4 * NB)
-        absv(1, 1, "A")
-        A([x1], [("D1", 0, 1)], T.D1[:, 0:80:5], n1q, AF.Copy)
-        keys(1, 1, "A", "KA1")
-        for v in range(2):
-            gat(0, v, "B")
-            absv(0, v, "B")
-            keys(0, v, "B", "KB0")
-        gat(1, 0, "B")
-        absv(1, 0, "B")
-        keys(1, 0, "B", "KB1")
-        gat(1, 1, "B", 0, NB - NL)
-        absv(1, 1, "B", 0, NB - NL)
-        gat(1, 1, "B", NB - NL, NB)
-        absv(1, 1, "B", NB - NL, NB)
-        A(["KB0"], [("K0S1", NB, 128)], T.K0S1[:, NB:128], T.KB0[:, 256:256 + 2 * NC:2], AF.Copy)
-        A(["KB0"], [("K0S1", 0, NB)], T.K0S1[:, 0:NB], T.KB0[:, 0:NB], AF.Copy)
-        keys(1, 1, "B", "KB1")
-        if t == 0:
-            lastconsts()
-            n0steps(T[n0q][:], [n0q])
-        best(0)
-        V("tt", ["KB0", ("K0S1", NB, 128)], [("km1", NB, 128)], T.km1[:, NB:128], T.KB0[:, 257:256 + 2 * NC:2], T.K0S1[:, NB:128], OP.min)
-        site(0, 0)
-        site(0, 1)
-        best(1)
-        accept()
-        if t < 3:
-            sn = "ST%d" % (t + 1)
-            newsrc()
-            newlists(T[sn][:, 0:256], [(sn, 0, 256)])
-            wn = "W%d" % (t + 1)
-            A([(sn, 0, 256)], [(wn, 0, 256)], T[wn][:, 0:256], T[sn][:, 0:256], AF.Copy)
-            send(t + 1, T.cores[(rank - 1 - (t + 1) % (NR_ - 1)) % NR_])
-            newnx(T[m0][:], [m0])
-            swap("MI1", lambda x: T[m0][:, x:16:2], [m0])
-            newf(T.F[:], ["F"])
-            V("tt", [("D0", 4, 5), "AS"], ["AS"], T.AS[:], acc, T.AS[:], OP.add)
-            for b in range(8):
-                mm(["B32", "AS"], ["MI2"], T.MI2[:, 0:2], T.B32[:], T.AS[:, 2 * b:2 * b + 2], b == 0, b == 7)
-            V("cp", ["MI1"], [mt], T[mt][:], T.MI1[:, 0:16])
-            n0steps(T[m0][:], [m0])
-            V("cp", ["MI2"], ["AI"], T.AI[:], T.MI2[:, 0:2])
-            V("ts", ["AI"], ["AI"], T.AI[:], T.AI[:], 7, None, OP.bitwise_and)
-            V("cp", ["AI"], ["AFl"], T.AFl[:], T.AI[:])
-            for x in range(2):
-                V("ts", ["AFl", "F"], [("FT", x, x + 1)], T.FT[:, x:16:2], T.F[:, x:16:2], T.AFl[:, x:x + 1], 32.0, OP.subtract, OP.mult)
+            for h in range(2):
+                mm(["IB", "L%d" % c], "AL", T.AL[:, c:256:2], wide("IB", h), T["L%d" % c][0:64, 128 * h:128 * h + 128],
+                   False, c == 1 and h == 1)
+
+    def lists(s, t, c):
+        w, n = "W%d%d" % (s, t), ("N1t" if c else "N0t%d" % s)
+        A([(w, 256, 512), n], ["L%d" % c], T["L%d" % c][:], T[w][:, 256:512].indirect(T[n][:, 0:16]), AF.Copy)
+
+    def offsets(bank, p0, q0, o, o0, n, i0):
+        ib, ri = T.IO[:, i0:i0 + n], ("IO", i0, i0 + n)
+        return [lambda: V("tt", [bank, "ODD"], [ri], ib, T[bank][:, p0:p0 + n], T.ODD[:, q0:q0 + n], OP.mult),
+                lambda: V("ts", [ri], [ri], ib, ib, 2, 4095, OP.arith_shift_right, OP.bitwise_and),
+                lambda: move(T[o][:, o0:o0 + n], ib, n, [ri], [(o, o0, o0 + n)])]
+
+    def move(out, in_, n, r, w):
+        if begun:
+            op("G", lambda: g.affine_select(out, in_, [[0, n]], OP.is_ge, 0.0, 0, 0), r, w)
         else:
-            newnx(T.ZO[:, 1:256:16], [("ZO", 1, 2)])
-            newf(T.ZO[:, 0:256:16], [("ZO", 0, 1)])
-            newlists(T.OUT[:], ["OUT"])
-            dma("S", T.yr[:], T.OUT[:], ["OUT"], ())
-            V("tr", ["ZO"], ["ZR"], T.ZR[:], T.ZO[:])
-            dma("A", T.yf[:], T.ZR[0:128:16, :], ["ZR"], ())
-            dma("S", T.yn[:], T.ZR[1:128:16, :], ["ZR"], ())
+            V("cp", r, w, out, in_)
+
+    def mix(*chains):
+        for k in range(max(len(c) for c in chains)):
+            for c in chains:
+                if k < len(c):
+                    c[k]()
+
+    def head1(s, t):
+        recv(s, t)
+        lists(s, t, 0)
+        pos1(0, 0, True)
+        pos1(0, 1, False)
+
+    def second():
+        V("tr", ["L0"], ["NT"], T.NT[64:128, :], T.L0[64:128, :])
+        for b in range(2):
+            for e in range(2):
+                k = 128 * (2 * b + e)
+                mm(["SN", "NT"], "N1", T.N1[:, b:16:2], T.SN[64:128, k:k + 128], T.NT[64:128, 16 * e:256:32], e == 0, e == 1)
+
+    def head2(s):
+        do = "DO%d" % s
+        o = offsets("PO0", 0, 4 * NC, "OV%d" % s, 0, 2 * NV, 0)
+        o[0]()
+        V("tt", ["N1", (do, 1, 2)], [(do, 0, 1)], T[do][:, 0:80:5], T[do][:, 1:80:5], T.N1[:, 0:16], OP.subtract)
+        V("cp", ["N1"], ["N1t"], T.N1t[:], T.N1[:, 0:16])
+        o[1]()
+        V("cp", ["N1"], [(do, 1, 2)], T[do][:, 1:80:5], T.N1[:, 0:16])
+        o[2]()
+
+    def head3(s, t):
+        lists(s, t, 1)
+        pos1(1, 1, False)
+        pos1(1, 0, True)
+
+    def head4(s):
+        mix(*[offsets("PO1", k, k, "OC%d" % s, k, 2 * NC, 2 * NV + k) for k in (0, 2 * NC)])
+
+    def head5(s):
+        return offsets("PO1", 4 * NC, 4 * NC, "OV%d" % s, 2 * NV, 2 * NV, 2 * NV + 4 * NC)
+
+    def gat(s, c, v, a=0, b=NV):
+        d, o, k = "D%d%d" % (c, v), "OV%d" % s, NV * (2 * c + v)
+        if a == b:
+            return
+        V("tt", ["S%d" % s, "XE%d" % s, (o, k + a, k + b)], [(d, a, b)], T[d][:, 16 * a:16 * b],
+          T["S%d" % s][:, 0:4096].indirect(T[o][:, k + a:k + b]), T["XE%d" % s][:, 16 * a:16 * b], OP.subtract)
+
+    def neg(c, v, a=0, b=NV):
+        d, r = "D%d%d" % (c, v), "R%d%d" % (c, v)
+        V("ts", [(d, a, b)], [(r, a, b)], T[r][:, 16 * a:16 * b], T[d][:, 16 * a:16 * b], 0.0, -2.0, OP.min, OP.mult)
+
+    def size(a, b):
+        A([("D11", a, b)], [("D11", a, b)], T.D11[:, 16 * a:16 * b], T.D11[:, 16 * a:16 * b], AF.Abs)
+
+    def keys(s, b, c, v, stop=False):
+        d, l, K = "%s%d%d" % (b, c, v), ("LH" if v else "LG"), "K%d" % s
+        for k in range(15 + v):
+            mm([(l, k, k + 1), d], K, T[K][:, c:2 * NV:2], T[l][:, 128 * k:128 * k + 128], T[d][:, k:16 * NV:16],
+               d == "D00" and k == 0, stop and k == 14 + v)
+
+    def cslots(s, a, b):
+        for i in range(a, b):
+            A(["S%d" % s, "OC%d" % s, "X%d" % s], [("CD", i, i + 1)], T.CD[:, 64 * i:64 * i + 64],
+              T["S%d" % s][:, 0:4096].indirect(T["OC%d" % s][:, 4 * i:4 * i + 4]), AF.Abs, bias=T["X%d" % s][:, NV + i:NV + i + 1], scale=-1.0)
+
+    def keysc(s, a, b, stop=False):
+        K = "K%d" % s
+        for v in range(2):
+            l = "LH" if v else "LG"
+            for k in range(15 + v):
+                mm([(l, k, k + 1), ("CD", a, b)], K, T[K][:, 2 * (NV + a):2 * (NV + b)], T[l][:, 128 * k:128 * k + 128],
+                   T.CD[:, 64 * a + 16 * v + k:64 * b:32], False, stop and v == 1 and k == 15)
+
+    def penalty(s):
+        V("ts", ["AR"], ["PN"], T.PN[:], T.AR[:], 127.5, None, OP.is_gt)
+        for x in (slice(0, 2 * NV, 2), slice(1, 2 * NV, 2), slice(2 * NV, 256)):
+            mm(["P22", "PN"], "K%d" % s, T["K%d" % s][:, x], T.P22[:], T.PN[:, x])
+
+    def best(s):
+        K = "K%d" % s
+        return [lambda: (A([K], ["K0S"], T.K0S[:], T[K][:, 0:256:2], AF.Identity, bias=-16.0),
+                         V("tt", [K, "K0S"], ["km"], T.km[:], T[K][:, 1:256:2], T.K0S[:], OP.min)),
+                lambda: V("tr", ["km"], ["XT"], T.XT[:], T.km[:]),
+                lambda: V("scan", ["RS", "XT"], ["Y"], T.Y[:], T.RS[:], T.XT[:], BIG, OP.add, OP.min)]
+
+    def finish(s, t, slots):
+        sel = select(s, t)
+        return (best(s) + [swap] + sel[:2] + [lambda: (sel[2](), slots(), site())] + sel[3:5]
+                + [lambda: (sel[5](), gap(s)), delta, lambda: newlists(s, t)])
+
+    def swap():
+        for h in range(2):
+            V("ts", ["Y"], [("YH", h, h + 1)], T.YH[:, 4 * h:4 * h + 4], T.Y[:, 15 + 16 * h:128:32], 31.0, None, OP.add)
+        for b in range(2):
+            mm(["SW", "YH"], "SM", T.SM[:, b:16:2], T.SW[:, 128 * b:128 * b + 128], T.YH[:], True, True)
+
+    def select(s, t):
+        dz, do, w = "DZ%d" % s, "DO%d" % s, "W%d%d" % (s, t)
+        key = T[do][:, 4:80:5]
+        return [
+            lambda: (V("cp", ["SM"], [(do, 4, 5)], key, T.SM[:, 0:16]),
+                     V("tt", ["SM", "FT%d" % s], [(dz, 3, 4)], T[dz][:, 3:80:5], T.SM[:, 0:16], T["FT%d" % s][:], OP.is_lt)),
+            lambda: (V("ts", [(do, 4, 5)], ["K31"], T.K31[:], key, 31, None, OP.bitwise_and),
+                     V("ts", [(do, 4, 5)], [("U", 1, 2)], T.U[:, 16:32], key, 0x7FFFFFE0, None, OP.bitwise_and)),
+            lambda: (V("ts", ["K31"], [(dz, 1, 2)], T[dz][:, 1:80:5], T.K31[:], 16.0, None, OP.is_lt),
+                     move(T.CODE[:], T.K31[:], 16, ["K31"], ["CODE"]),
+                     move(T[dz][:, 83:160:5], T[dz][:, 3:80:5], 16, [(dz, 3, 4)], [(dz, 5, 6)])),
+            lambda: V("scan", [(dz, 0, 5), (do, 0, 5)], ["FS"], T.FS[:], T[dz][:, 0:80], T[do][:, 0:80], 0.0, OP.mult, OP.add),
+            lambda: (V("cp", ["FS"], ["SEL"], T.SEL[:], T.FS[:, 3:80:5]),
+                     V("ts", ["FS"], [("U", 0, 1)], T.U[:, 0:16], T.FS[:, 4:80:5], 5, 255, OP.arith_shift_right, OP.bitwise_and)),
+            lambda: V("cp", [w, "SEL"], ["BS"], T.BS[:], T[w][:, 0:768].indirect(T.SEL[:, 0:16]))]
+
+    def site():
+        A(["MK", "CODE"], ["OH"], T.OH[:], T.MK[:, 0:32].indirect(T.CODE[:, 0:16]), AF.Copy)
+
+    def distance():
+        A(["AL"], ["AR"], T.AR[:], T.AL[:, 0:256], AF.Abs, bias=-4223.5)
+
+    def gap(s):
+        w = "W%d0" % s
+        mm(["Bw", (w, 0, 256)], "DD", T.DD[:, 0:256], wide("Bw", 0), T[w][0:64, 0:256], True)
+        mm(["NB", "BS"], "DD", T.DD[:, 0:256], wide("NB", 0), T.BS[0:64, :], False, True)
+        mm(["I", "BS"], "N1", T.N1[:, 256:512], T.I[:], T.BS[:], True, True)
+
+    def delta():
+        V("tt", ["DD", "OH"], ["MD"], T.MD[:], T.DD[:, 0:256], T.OH[:], OP.mult)
+
+    def newlists(s, t):
+        if t < 3:
+            w = "W%d%d" % (s, t + 1)
+            V("tt", ["N1", "MD"], [(w, 0, 256)], T[w][:, 0:256], T.N1[:, 256:512], T.MD[:], OP.add)
+            send(s, t + 1)
+        else:
+            o = "OUT%d" % s
+            V("tt", ["N1", "MD"], [o], T[o][0:64, :], T.N1[0:64, 256:512], T.MD[0:64, :], OP.add)
+            dma("S", T.yr[half(s), :], T[o][0:64, :], [o], ())
+
+    def tally(s):
+        dz = "DZ%d" % s
+        mm(["B2x", (dz, 3, 4)], "SM", T.SM[:, 32:48], T.B2x[0:64, :], T[dz][0:64, 3:80:5], True, True)
+
+    def post1(s, t):
+        dz, do, to = "DZ%d" % s, "DO%d" % s, "TO%d" % s
+        x, rx = T[do][:, 1:160:5], [(do, 1, 2), (do, 5, 6)]
+
+        def middle():
+            V("tt", ["E1", (dz, 3, 6)], ["E2"], T.E2[:], T.E1[:], T[dz][:, 3:160:5], OP.mult)
+            if t < 3:
+                V("scan", ["SM", "ones", to], [(to, t, t + 1)], T[to][:, 32 * t:32 * t + 32], T.ones[:, 0:32], T.SM[:, 32:64],
+                  T[to][:, 32 * t - 1:32 * t] if t else 0.0, OP.mult, OP.add)
+                move(T.AI[:], T[to][:, 32 * t + 16:32 * t + 32], 16, [to], ["AI"])
+        return [lambda: V("tt", ["U"] + rx, ["E1"], T.E1[:], T.U[:], x, OP.subtract), middle,
+                lambda: V("tt", ["E2"] + rx, rx, x, T.E2[:], x, OP.add)]
+
+    def post2(s, t):
+        do = "DO%d" % s
+        if t < 3:
+            move(T["N0t%d" % s][:], T[do][:, 1:80:5], 16, [(do, 1, 2)], ["N0t%d" % s])
+            numbers(s, t + 1)
+
+    def post3(s, t):
+        do = "DO%d" % s
+        if t < 3:
+            return [lambda: V("ts", ["AI"], ["AM"], T.AM[:], T.AI[:], 255, None, OP.bitwise_and),
+                    lambda: V("tt", [(do, 5, 6), "AM"], ["FT%d" % s], T["FT%d" % s][:], T[do][:, 81:160:5], T.AM[:], OP.subtract)]
+        zi, zt, bank = "ZI%d" % s, "ZT%d" % s, "PO%d" % s
+
+        def tables():
+            V("cp", [(do, 1, 2)], [(zi, 0, 1)], T[zi][0:64, :], T[do][0:64, 1:80:5])
+            V("ts", [(do, 5, 6)], [(zi, 1, 2)], T[zi][64:128, :], T[do][64:128, 81:160:5], 1.0 / 32, None, OP.mult)
+
+        def rows():
+            V("tt", [zi, "EX", "MK"], ["ZX"], T.ZX[:], T[zi][:, 0:16].indirect(T.EX[:, 0:16]), T.MK[:], OP.mult)
+
+        def store():
+            mm(["BD", "ZX"], bank, T[bank][:, 0:256], T.BD[:], T.ZX[:], True, True)
+            A([bank], [zt], T[zt][:], T[bank][:, 0:256], AF.Copy)
+            dma("SA"[s], T.yn[4 * s:4 * s + 4, :], T[zt][0:64:16, :], [zt], ())
+            dma("SA"[s], T.yf[4 * s:4 * s + 4, :], T[zt][64:128:16, :], [zt], ())
+        return [tables, rows, store]
+
+    mix(mass(0), mass(1))
+    pos0(0)
+    keyconsts()
+    head1(0, 0)
+    for h in range(2):
+        dma("S", T.S1[half(h), :], T.prof[half(1), :], [("W00", 256, 512)], [("S1", h, h + 1)])
+    second()
+    head2(0)
+    head3(0, 0)
+    gat(0, 0, 0, 0, G0)
+    head4(0)
+    for p in range(8):
+        s, y = p % 2, 1 - p % 2
+        tail, ty = p >= 1, (p - 1) // 2
+        head, th = p < 7, (p + 1) // 2
+        allowed_mm()
+        gat(s, 0, 0, 0 if tail else G0, NV)
+        cslots(s, 0, A1)
+        keys(s, "D", 0, 0)
+        later = post1(y, ty) + post3(y, ty) if tail else [lambda: None] * 5
+        h5, cut = head5(s), [NV * k // 6 for k in range(7)]
+        piece = [lambda k=k: neg(0, 0, cut[k], cut[k + 1]) for k in range(6)]
+        part = [lambda a=a, b=b: gat(s, 0, 1, a, b) for a, b in ((0, GA), (GA, GB), (GB, GC), (GC, NV))]
+        mix([lambda: (h5[0](), piece[0]()), lambda: (h5[1](), h5[2](), distance()), piece[1], piece[2], part[0], piece[3], piece[4],
+             lambda: (piece[5](), keys(s, "R", 0, 0)), lambda: penalty(s), part[1], part[2], later[0], part[3]],
+            finish(y, ty, lambda: cslots(s, A1, A2)) if tail else [lambda: cslots(s, A1, A2), lastconsts])
+        begun.append(p)
+        if tail and ty < 3:
+            tally(y)
+        if head:
+            pos0(y)
+        cslots(s, A2, CB)
+        keysc(s, 0, CB)
+        keys(s, "D", 0, 1)
+        later[1]()
+        neg(0, 1)
+        later[2]()
+        keys(s, "R", 0, 1)
+        if tail:
+            post2(y, ty)
+        gat(s, 1, 0)
+        keys(s, "D", 1, 0)
+        later[3]()
+        neg(1, 0)
+        cslots(s, CB, A4)
+        if head:
+            later[4]()
+        if head:
+            head1(y, th)
+        gat(s, 1, 1, 0, G2)
+        if head:
+            second()
+        keys(s, "R", 1, 0)
+        gat(s, 1, 1, G2, G3)
+        if head:
+            head2(y)
+        cslots(s, A4, A5)
+        if head:
+            head3(y, th)
+        size(0, G3)
+        gat(s, 1, 1, G3, NV)
+        if p == 0:
+            fit(0)
+        if head:
+            head4(y)
+        if p == 0:
+            fit(1)
+            fit(2)
+        cslots(s, A5, NC)
+        keysc(s, CB, NC)
+        size(G3, NV)
+        keys(s, "D", 1, 1, True)
+    steps = finish(1, 3, lambda: None)
+    mix(later[4:5] + steps[:1] + later[5:] + steps[1:10] + post1(1, 3) + post3(1, 3) + steps[10:])
 
     known = {}
     for o in ops:

@@ -1,10 +1,11 @@
 from concourse.mybir import AluOpType as OP, ActivationFunctionType as AF
 
-NV = 72
+NV = 74
 NC = 128 - NV
-GA, GB, GC = 24, 32, 44
-G0, G2, G3 = 14, 26, 32
-A1, A2, CB, A4, A5 = 5, 17, 28, 44, 54
+GA, GB = 22, 64
+GL = 12
+G0, G1, G2, G3 = 14, 30, 30, 38
+A1, A2, CB, A4, A5 = 5, 18, 22, 45, 50
 BIG = float(2 ** 26)
 BF, F32, I32, U16 = "bfloat16", "float32", "int32", "uint16"
 
@@ -12,20 +13,20 @@ SCRATCH = {}
 for _n, _w, _d in (
         ("ip", 1, I32), ("ic", 8, I32), ("CF", 24, F32), ("RI", 512, I32), ("TBi", 32, I32), ("TB", 32, U16), ("NI", 32, I32),
         ("ZF", 32, I32), ("ZG", 32, F32), ("ZH", 32, F32), ("CI", 16, F32),
-        ("jm1", 128, BF), ("gw", 192, BF), ("g4", 128, BF), ("c64", 128, BF), ("g32", 256, BF), ("WM", 128, BF), ("KC", 128, BF),
+        ("jm1", 128, BF), ("gw", 192, BF), ("g4", 128, BF), ("c64", 128, BF), ("g32", 256, BF), ("WM", 128, BF), ("KC", 128, BF), ("YH", 8, F32),
         ("ones", 512, BF), ("Bw", 192, BF), ("TRI", 192, BF), ("HN", 192, BF), ("IB", 192, BF), ("NB", 192, BF),
-        ("P22", 128, BF), ("I", 128, BF), ("B2x", 128, BF), ("SW", 256, F32), ("SN", 512, BF), ("NT", 256, BF),
+        ("P22", 128, BF), ("B2x", 128, BF), ("SW", 256, F32), ("SN", 512, BF), ("NT", 256, BF),
         ("LG", 15 * 128, BF), ("LH", 16 * 128, BF), ("BH", 128, BF),
-        ("BX", 256, BF), ("MK", 256, BF), ("BD", 128, F32), ("EX", 16, U16), ("ZX", 256, F32), ("RS", 128, F32), ("YH", 8, F32),
+        ("BX", 256, BF), ("MK", 256, BF), ("BD", 128, F32), ("EX", 16, U16), ("ZX", 256, F32), ("RS", 128, F32),
         ("XT", 128, F32), ("AM", 16, I32), ("ODD", 4 * NC + 2 * NV, F32), ("IO", 4 * NC + 4 * NV, I32),
         ("CD", 64 * NC, BF), ("K0S", 128, F32), ("km", 128, F32), ("Y", 128, F32),
-        ("FS", 80, I32), ("K31", 16, I32), ("U", 32, I32), ("E1", 32, F32), ("E2", 32, F32), ("AI", 16, I32),
-        ("SEL", 16, U16), ("CODE", 16, U16), ("N1t", 16, U16), ("BS", 256, BF), ("OH", 256, BF), ("MD", 256, BF),
+        ("FS", 80, I32), ("KS", 8, I32), ("IH", 256, BF), ("AC", 32, BF), ("U", 32, I32), ("E1", 32, F32), ("E2", 32, F32), ("AI", 16, I32),
+        ("SEL", 16, U16), ("CODE", 8, U16), ("N1t", 16, U16), ("BS", 256, BF), ("OH", 128, BF), ("MD", 128, BF),
         ("AR", 256, BF), ("PN", 256, BF), ("L0", 256, BF), ("L1", 256, BF)):
     SCRATCH[_n] = ("sbuf", [128, _w], _d)
 for _s in range(2):
     for _n, _w, _d in (("S", 4096, BF), ("X", 128, BF), ("XE", 16 * NV, BF), ("OV", 4 * NV, U16), ("OC", 4 * NC, U16),
-                       ("DZ", 160, BF), ("DO", 160, I32), ("N0t", 16, U16), ("FT", 16, F32), ("TO", 96, F32),
+                       ("DZ", 80, I32), ("DO", 80, I32), ("XO", 32, I32), ("N0t", 16, U16), ("FT", 16, F32), ("TO", 96, F32),
                        ("CM", 4 * NC + 2 * NV, BF), ("ZB", 128, BF),
                        ("OUT", 256, F32), ("ZI", 16, F32), ("ZT", 256, F32)):
         SCRATCH[_n + str(_s)] = ("sbuf", [128, _w], _d)
@@ -190,6 +191,8 @@ def rank_program(g, core, T, topo):
     bits(7, 0, 32)
     V("ts", [("CF", 7, 8)], [("CF", 1, 2)], C(1), C(7), 0.0, 256.0, OP.is_equal, OP.mult)
     col(14, 6, 1, 0)
+    col(23, 2, -1, 1)
+    col(22, 2, -31.0 / 32, 1)
     for k, src, r, m in ((4, T.ic[:, 3:4], ("ic", 3, 4), 16.0), (15, T.ic[:, 7:8], ("ic", 7, 8), 1.0), (16, C(2), ("CF", 2, 3), 16.0)):
         V("ts", [r, ("CF", 7, 8)], [("CF", k, k + 1)], C(k), src, m, C(7), OP.mult, OP.add)
     V("cp", ["ip"], [("CF", 17, 18)], C(17), T.ip[:])
@@ -213,6 +216,9 @@ def rank_program(g, core, T, topo):
            ["BH"], [("LH", k, k + 1)])
     numbers(1, 0)
     for s in range(2):
+        for k, c in ((0, 0), (2, 1), (4, 416)):
+            iota([("DZ%d" % s, k, k + 1)], T["DZ%d" % s][:, k:80:5], [[0, 16]], c, 0, False)
+    for s in range(2):
         for k in range(16):
             A(["X%d" % s], [("XE%d" % s, k, k + 1)], T["XE%d" % s][:, k:16 * NV:16], T["X%d" % s][:, 0:NV], AF.Copy)
     J = T.jm1[:, 0:128]
@@ -232,16 +238,15 @@ def rank_program(g, core, T, topo):
                 V("ts", ["c64", "CF"], [("SN", k, k + 1)], T.SN[:, 128 * k:128 * k + 128], T.c64[:], C(20 + b), 16.0 * e,
                   OP.subtract, OP.is_equal)
         V("ts", [rnum, "CF"], ["P22"], T.P22[:], num, C(16), float(2 ** 22), OP.is_equal, OP.mult)
-        V("ts", [rnum, "CF"], ["I"], T.I[:], num, C(17), None, OP.is_equal)
+        V("ts", [rnum, "CF"], [("IH", 0, 1)], T.IH[:, 0:128], num, C(17), C(23), OP.is_equal, OP.mult)
+        V("ts", [rnum, "CF"], [("IH", 1, 2)], T.IH[:, 128:256], T.W00[:, 576:704], C(17), None, OP.is_equal)
         V("set", (), ["SM"], T.SM[:, 48:64], 0.0)
-        V("ts", ["gw", "CF"], ["BD"], T.BD[:], T.gw[:, 64:192], C(14), None, OP.is_equal)
+        V("ts", ["gw", "CF"], ["BD"], T.BD[:], T.gw[:, 64:192], C(14), C(22), OP.is_equal, OP.mult)
         V("cp", [rnum], ["EX"], T.EX[:], T.W00[:, 512:528])
         for b in range(2):
             V("ts", ["c64", "CF"], [("SW", b, b + 1)], T.SW[:, 128 * b:128 * b + 128], T.c64[:], C(18 + b), None, OP.is_equal)
         for s in range(2):
-            dz, do = "DZ%d" % s, "DO%d" % s
-            for k, c in ((0, 0.0), (2, 1.0), (4, 416.0)):
-                A(["ones"], [(dz, k, k + 1)], T[dz][:, k:80:5], T.ones[:, 0:16], AF.Copy, scale=c)
+            do = "DO%d" % s
             V("ts", ["CI", "CF"], [(do, 2, 3)], T[do][:, 2:80:5], T.CI[:], -1.0, C(8), OP.mult, OP.add)
             V("cp", ["CI"], [(do, 3, 4)], T[do][:, 3:80:5], T.CI[:])
         for k in range(15):
@@ -260,8 +265,7 @@ def rank_program(g, core, T, topo):
         if step == 1:
             V("tr", ["ZG"], ["ZH"], T.ZH[:], T.ZG[:])
         for s in range(2 if step == 2 else 0):
-            do = "DO%d" % s
-            V("cp", ["ZH"], [(do, 5, 6)], T[do][:, 81:160:5], T.ZH[:, 16 * s:16 * s + 16])
+            V("cp", ["ZH"], [("XO%d" % s, 1, 2)], T["XO%d" % s][:, 16:32], T.ZH[:, 16 * s:16 * s + 16])
             V("cp", ["ZH"], ["FT%d" % s], T["FT%d" % s][:], T.ZH[:, 16 * s:16 * s + 16])
 
     def wide(name, h):
@@ -318,8 +322,8 @@ def rank_program(g, core, T, topo):
                 lambda: V("ts", [ri], [ri], ib, ib, 2, 4095, OP.arith_shift_right, OP.bitwise_and),
                 lambda: move(T[o][:, o0:o0 + n], ib, n, [ri], [(o, o0, o0 + n)])]
 
-    def move(out, in_, n, r, w):
-        if begun:
+    def move(out, in_, n, r, w, urgent=False):
+        if begun and not urgent:
             op("G", lambda: g.affine_select(out, in_, [[0, n]], OP.is_ge, 0.0, 0, 0), r, w)
         else:
             V("cp", r, w, out, in_)
@@ -347,10 +351,10 @@ def rank_program(g, core, T, topo):
         do = "DO%d" % s
         o = offsets("PO0", 0, 4 * NC, "OV%d" % s, 0, 2 * NV, 0)
         o[0]()
-        V("tt", ["N1", (do, 1, 2)], [(do, 0, 1)], T[do][:, 0:80:5], T[do][:, 1:80:5], T.N1[:, 0:16], OP.subtract)
         V("cp", ["N1"], ["N1t"], T.N1t[:], T.N1[:, 0:16])
+        V("tt", ["N1", (do, 1, 2)], [(do, 0, 1)], T[do][:, 0:80:5], T.N1[:, 0:16], T[do][:, 1:80:5], OP.subtract)
         o[1]()
-        V("cp", ["N1"], [(do, 1, 2)], T[do][:, 1:80:5], T.N1[:, 0:16])
+        V("cp", ["N1"], [("XO%d" % s, 0, 1)], T["XO%d" % s][:, 0:16], T.N1[:, 0:16])
         o[2]()
 
     def head3(s, t):
@@ -391,7 +395,7 @@ def rank_program(g, core, T, topo):
 
     def keysc(s, a, b, stop=False):
         K = "K%d" % s
-        for v in range(2):
+        for v in range(2 if a < b else 0):
             l = "LH" if v else "LG"
             for k in range(15 + v):
                 mm([(l, k, k + 1), ("CD", a, b)], K, T[K][:, 2 * (NV + a):2 * (NV + b)], T[l][:, 128 * k:128 * k + 128],
@@ -411,8 +415,8 @@ def rank_program(g, core, T, topo):
 
     def finish(s, t, slots):
         sel = select(s, t)
-        return (best(s) + [swap] + sel[:2] + [lambda: (sel[2](), slots(), site())] + sel[3:5]
-                + [lambda: (sel[5](), gap(s)), delta, lambda: newlists(s, t)])
+        return (best(s) + [swap, sel[0], lambda: (sel[1](), slots(), site())] + sel[2:4]
+                + [lambda: (sel[4](), gap(), tally(t)), delta, lambda: newlists(s, t)])
 
     def swap():
         for h in range(2):
@@ -426,74 +430,87 @@ def rank_program(g, core, T, topo):
         return [
             lambda: (V("cp", ["SM"], [(do, 4, 5)], key, T.SM[:, 0:16]),
                      V("tt", ["SM", "FT%d" % s], [(dz, 3, 4)], T[dz][:, 3:80:5], T.SM[:, 0:16], T["FT%d" % s][:], OP.is_lt)),
-            lambda: (V("ts", [(do, 4, 5)], ["K31"], T.K31[:], key, 31, None, OP.bitwise_and),
-                     V("ts", [(do, 4, 5)], [("U", 1, 2)], T.U[:, 16:32], key, 0x7FFFFFE0, None, OP.bitwise_and)),
-            lambda: (V("ts", ["K31"], [(dz, 1, 2)], T[dz][:, 1:80:5], T.K31[:], 16.0, None, OP.is_lt),
-                     move(T.CODE[:], T.K31[:], 16, ["K31"], ["CODE"]),
-                     move(T[dz][:, 83:160:5], T[dz][:, 3:80:5], 16, [(dz, 3, 4)], [(dz, 5, 6)])),
+            lambda: (V("ts", [(do, 4, 5)], [(dz, 1, 2)], T[dz][:, 1:80:5], key, 4, 1, OP.arith_shift_right, OP.bitwise_and),
+                     [V("ts", [(do, 4, 5)], [("KS", h, h + 1)], T.KS[half(h), :], T[do][half(h), 4 + 40 * h:40 + 40 * h:5], 15, None,
+                        OP.bitwise_and) for h in range(2)],
+                     V("ts", [(do, 4, 5)], [("U", 1, 2)], T.U[:, 16:32], key, 0x7FFFFFE0, None, OP.bitwise_and),
+                     move(T.CODE[:], T.KS[:], 8, ["KS"], ["CODE"]),
+                     [move(T.AC[:, 16 * k:16 * k + 16], T[dz][:, 3:80:5], 16, [(dz, 3, 4)], [("AC", k, k + 1)]) for k in range(2)]),
             lambda: V("scan", [(dz, 0, 5), (do, 0, 5)], ["FS"], T.FS[:], T[dz][:, 0:80], T[do][:, 0:80], 0.0, OP.mult, OP.add),
             lambda: (V("cp", ["FS"], ["SEL"], T.SEL[:], T.FS[:, 3:80:5]),
                      V("ts", ["FS"], [("U", 0, 1)], T.U[:, 0:16], T.FS[:, 4:80:5], 5, 255, OP.arith_shift_right, OP.bitwise_and)),
-            lambda: V("cp", [w, "SEL"], ["BS"], T.BS[:], T[w][:, 0:768].indirect(T.SEL[:, 0:16]))]
+            lambda: (V("cp", [w, "SEL"], ["BS"], T.BS[:], T[w][:, 0:768].indirect(T.SEL[:, 0:16])) if (s, t) == (1, 3) else
+                     A([w, "SEL"], ["BS"], T.BS[:], T[w][:, 0:768].indirect(T.SEL[:, 0:16]), AF.Copy))]
 
     def site():
-        A(["MK", "CODE"], ["OH"], T.OH[:], T.MK[:, 0:32].indirect(T.CODE[:, 0:16]), AF.Copy)
+        A(["MK", "CODE"], ["OH"], T.OH[:], T.MK[:, 0:16].indirect(T.CODE[:, 0:8]), AF.Copy)
 
     def distance():
         A(["AL"], ["AR"], T.AR[:], T.AL[:, 0:256], AF.Abs, bias=-4223.5)
 
-    def gap(s):
+    def own(s):
         w = "W%d0" % s
-        mm(["Bw", (w, 0, 256)], "DD", T.DD[:, 0:256], wide("Bw", 0), T[w][0:64, 0:256], True)
-        mm(["NB", "BS"], "DD", T.DD[:, 0:256], wide("NB", 0), T.BS[0:64, :], False, True)
-        mm(["I", "BS"], "N1", T.N1[:, 256:512], T.I[:], T.BS[:], True, True)
+        for h in range(2):
+            mm(["Bw", (w, 0, 256)], "DD", T.DD[:, 0:128], wide("Bw", h), T[w][0:64, 128 * h:128 * h + 128], h == 0)
+
+    def gap():
+        for h in range(2):
+            mm(["NB", "BS"], "DD", T.DD[:, 0:128], wide("NB", h), T.BS[0:64, 128 * h:128 * h + 128], False, h == 1)
 
     def delta():
-        V("tt", ["DD", "OH"], ["MD"], T.MD[:], T.DD[:, 0:256], T.OH[:], OP.mult)
+        V("tt", ["DD", "OH"], ["MD"], T.MD[:], T.DD[:, 0:128], T.OH[:], OP.mult)
+        for h in range(2):
+            mm(["IH", "MD"], "N1", T.N1[:, 256 + 128 * h:384 + 128 * h], T.IH[:, 128 * h:128 * h + 128], T.MD[:], True, True)
 
     def newlists(s, t):
         if t < 3:
             w = "W%d%d" % (s, t + 1)
-            V("tt", ["N1", "MD"], [(w, 0, 256)], T[w][:, 0:256], T.N1[:, 256:512], T.MD[:], OP.add)
+            V("tt", ["N1", "BS"], [(w, 0, 256)], T[w][:, 0:256], T.N1[:, 256:512], T.BS[:], OP.add)
             send(s, t + 1)
         else:
             o = "OUT%d" % s
-            V("tt", ["N1", "MD"], [o], T[o][0:64, :], T.N1[0:64, 256:512], T.MD[0:64, :], OP.add)
+            V("tt", ["N1", "BS"], [o], T[o][0:64, :], T.N1[0:64, 256:512], T.BS[0:64, :], OP.add)
             dma("S", T.yr[half(s), :], T[o][0:64, :], [o], ())
 
-    def tally(s):
-        dz = "DZ%d" % s
-        mm(["B2x", (dz, 3, 4)], "SM", T.SM[:, 32:48], T.B2x[0:64, :], T[dz][0:64, 3:80:5], True, True)
+    def tally(t):
+        if t < 3:
+            mm(["B2x", ("AC", 0, 1)], "SM", T.SM[:, 32:48], T.B2x[0:64, :], T.AC[0:64, 0:16], True, True)
 
     def post1(s, t):
-        dz, do, to = "DZ%d" % s, "DO%d" % s, "TO%d" % s
-        x, rx = T[do][:, 1:160:5], [(do, 1, 2), (do, 5, 6)]
+        xo, to = "XO%d" % s, "TO%d" % s
 
-        def middle():
-            V("tt", ["E1", (dz, 3, 6)], ["E2"], T.E2[:], T.E1[:], T[dz][:, 3:160:5], OP.mult)
+        def first():
+            V("tt", ["U", xo], ["E1"], T.E1[:], T.U[:], T[xo][:], OP.subtract)
             if t < 3:
                 V("scan", ["SM", "ones", to], [(to, t, t + 1)], T[to][:, 32 * t:32 * t + 32], T.ones[:, 0:32], T.SM[:, 32:64],
                   T[to][:, 32 * t - 1:32 * t] if t else 0.0, OP.mult, OP.add)
+
+        def middle():
+            V("tt", ["E1", "AC"], ["E2"], T.E2[:], T.E1[:], T.AC[:], OP.mult)
+            if t < 3:
                 move(T.AI[:], T[to][:, 32 * t + 16:32 * t + 32], 16, [to], ["AI"])
-        return [lambda: V("tt", ["U"] + rx, ["E1"], T.E1[:], T.U[:], x, OP.subtract), middle,
-                lambda: V("tt", ["E2"] + rx, rx, x, T.E2[:], x, OP.add)]
+
+        def last():
+            if t < 3:
+                V("tt", ["E2", xo], [xo], T[xo][:], T.E2[:], T[xo][:], OP.add)
+            for h in range(2 if t == 3 else 0):
+                V("tt", ["E2", xo], [("ZI%d" % s, h, h + 1)], T["ZI%d" % s][half(h), :], T.E2[half(h), 16 * h:16 * h + 16],
+                  T[xo][half(h), 16 * h:16 * h + 16], OP.add)
+        return [first, middle, last]
 
     def post2(s, t):
-        do = "DO%d" % s
+        do, xo = "DO%d" % s, "XO%d" % s
         if t < 3:
-            move(T["N0t%d" % s][:], T[do][:, 1:80:5], 16, [(do, 1, 2)], ["N0t%d" % s])
+            move(T["N0t%d" % s][:], T[xo][:, 0:16], 16, [xo], ["N0t%d" % s])
+            move(T[do][:, 1:80:5], T[xo][:, 0:16], 16, [xo], [(do, 1, 2)])
             numbers(s, t + 1)
 
     def post3(s, t):
-        do = "DO%d" % s
+        xo = "XO%d" % s
         if t < 3:
             return [lambda: V("ts", ["AI"], ["AM"], T.AM[:], T.AI[:], 255, None, OP.bitwise_and),
-                    lambda: V("tt", [(do, 5, 6), "AM"], ["FT%d" % s], T["FT%d" % s][:], T[do][:, 81:160:5], T.AM[:], OP.subtract)]
+                    lambda: V("tt", [xo, "AM"], ["FT%d" % s], T["FT%d" % s][:], T[xo][:, 16:32], T.AM[:], OP.subtract)]
         zi, zt, bank = "ZI%d" % s, "ZT%d" % s, "PO%d" % s
-
-        def tables():
-            V("cp", [(do, 1, 2)], [(zi, 0, 1)], T[zi][0:64, :], T[do][0:64, 1:80:5])
-            V("ts", [(do, 5, 6)], [(zi, 1, 2)], T[zi][64:128, :], T[do][64:128, 81:160:5], 1.0 / 32, None, OP.mult)
 
         def rows():
             V("tt", [zi, "EX", "MK"], ["ZX"], T.ZX[:], T[zi][:, 0:16].indirect(T.EX[:, 0:16]), T.MK[:], OP.mult)
@@ -503,7 +520,7 @@ def rank_program(g, core, T, topo):
             A([bank], [zt], T[zt][:], T[bank][:, 0:256], AF.Copy)
             dma("SA"[s], T.yn[4 * s:4 * s + 4, :], T[zt][0:64:16, :], [zt], ())
             dma("SA"[s], T.yf[4 * s:4 * s + 4, :], T[zt][64:128:16, :], [zt], ())
-        return [tables, rows, store]
+        return [lambda: None, rows, store]
 
     mix(mass(0), mass(1))
     pos0(0)
@@ -524,18 +541,15 @@ def rank_program(g, core, T, topo):
         gat(s, 0, 0, 0 if tail else G0, NV)
         cslots(s, 0, A1)
         keys(s, "D", 0, 0)
-        later = post1(y, ty) + post3(y, ty) if tail else [lambda: None] * 5
-        h5, cut = head5(s), [NV * k // 6 for k in range(7)]
-        piece = [lambda k=k: neg(0, 0, cut[k], cut[k + 1]) for k in range(6)]
-        part = [lambda a=a, b=b: gat(s, 0, 1, a, b) for a, b in ((0, GA), (GA, GB), (GB, GC), (GC, NV))]
-        mix([lambda: (h5[0](), piece[0]()), lambda: (h5[1](), h5[2](), distance()), piece[1], piece[2], part[0], piece[3], piece[4],
-             lambda: (piece[5](), keys(s, "R", 0, 0)), lambda: penalty(s), part[1], part[2], later[0], part[3]],
+        later = post1(y, ty) + post3(y, ty) if tail else [lambda: None] * 2 + [lambda k=k: fit(k) for k in range(3)]
+        h5, cut = head5(s), [NV * k // 5 for k in range(6)]
+        piece = [lambda k=k: neg(0, 0, cut[k], cut[k + 1]) for k in range(5)]
+        part = [lambda a=a, b=b: gat(s, 0, 1, a, b) for a, b in ((0, GA), (GA, GB), (GB, NV))]
+        mix([lambda: (h5[0](), piece[0]()), lambda: (h5[1](), h5[2](), distance()), piece[1], piece[2],
+             lambda: (part[0](), pos0(y) if head else None, own(y) if tail else None), piece[3], lambda: (piece[4](), keys(s, "R", 0, 0)), lambda: penalty(s),
+             lambda: None, part[1], lambda: (later[0](), part[2]())],
             finish(y, ty, lambda: cslots(s, A1, A2)) if tail else [lambda: cslots(s, A1, A2), lastconsts])
         begun.append(p)
-        if tail and ty < 3:
-            tally(y)
-        if head:
-            pos0(y)
         cslots(s, A2, CB)
         keysc(s, 0, CB)
         keys(s, "D", 0, 1)
@@ -548,37 +562,41 @@ def rank_program(g, core, T, topo):
         gat(s, 1, 0)
         keys(s, "D", 1, 0)
         later[3]()
-        neg(1, 0)
         cslots(s, CB, A4)
         if head:
-            later[4]()
-        if head:
             head1(y, th)
-        gat(s, 1, 1, 0, G2)
+        gat(s, 1, 1, 0, G1)
+        if head:
+            later[4]()
+        neg(1, 0)
+        gat(s, 1, 1, G1, G2)
         if head:
             second()
         keys(s, "R", 1, 0)
-        gat(s, 1, 1, G2, G3)
+        gat(s, 1, 1, G2, G3 if head else G2)
         if head:
             head2(y)
         cslots(s, A4, A5)
         if head:
             head3(y, th)
-        size(0, G3)
-        gat(s, 1, 1, G3, NV)
-        if p == 0:
-            fit(0)
         if head:
+            cslots(s, A5, NC)
+            keysc(s, CB, NC)
+            size(0, G3)
+            gat(s, 1, 1, G3, NV)
             head4(y)
-        if p == 0:
-            fit(1)
-            fit(2)
-        cslots(s, A5, NC)
-        keysc(s, CB, NC)
-        size(G3, NV)
+            size(G3, NV)
+        else:
+            cslots(s, A5, NC)
+            keysc(s, CB, NC)
+            size(0, G2)
+            for a, b in ((G2, NV - GL), (NV - GL, NV)):
+                gat(s, 1, 1, a, b)
+                size(a, b)
         keys(s, "D", 1, 1, True)
     steps = finish(1, 3, lambda: None)
-    mix(later[4:5] + steps[:1] + later[5:] + steps[1:10] + post1(1, 3) + post3(1, 3) + steps[10:])
+    one, two = post1(1, 3), post3(1, 3)
+    mix(later[4:5] + steps[:2] + later[5:] + [lambda: own(1)] + steps[2:8] + [one[0], steps[8], one[1], one[2], steps[9], two[1], steps[10], two[2]])
 
     known = {}
     for o in ops:

from concourse.mybir import AluOpType as OP, ActivationFunctionType as AF

NV = 74
NC = 128 - NV
GA, GB = 22, 64
GL = 12
G0, G1, G2, G3 = 14, 30, 30, 38
A1, A2, CB, A4, A5 = 5, 18, 22, 45, 50
BIG = float(2 ** 26)
BF, F32, I32, U16 = "bfloat16", "float32", "int32", "uint16"

SCRATCH = {}
for _n, _w, _d in (
        ("ip", 1, I32), ("ic", 8, I32), ("CF", 24, F32), ("RI", 512, I32), ("TBi", 32, I32), ("TB", 32, U16), ("NI", 32, I32),
        ("ZF", 32, I32), ("ZG", 32, F32), ("ZH", 32, F32), ("CI", 16, F32),
        ("jm1", 128, BF), ("gw", 192, BF), ("g4", 128, BF), ("c64", 128, BF), ("g32", 256, BF), ("WM", 128, BF), ("KC", 128, BF), ("YH", 8, F32),
        ("ones", 512, BF), ("Bw", 192, BF), ("TRI", 192, BF), ("HN", 192, BF), ("IB", 192, BF), ("NB", 192, BF),
        ("P22", 128, BF), ("B2x", 128, BF), ("SW", 256, F32), ("SN", 512, BF), ("NT", 256, BF),
        ("LG", 15 * 128, BF), ("LH", 16 * 128, BF), ("BH", 128, BF),
        ("BX", 256, BF), ("MK", 256, BF), ("BD", 128, F32), ("EX", 16, U16), ("ZX", 256, F32), ("RS", 128, F32),
        ("XT", 128, F32), ("AM", 16, I32), ("ODD", 4 * NC + 2 * NV, F32), ("IO", 4 * NC + 4 * NV, I32),
        ("CD", 64 * NC, BF), ("K0S", 128, F32), ("km", 128, F32), ("Y", 128, F32),
        ("FS", 80, I32), ("KS", 8, I32), ("IH", 256, BF), ("AC", 32, BF), ("U", 32, I32), ("E1", 32, F32), ("E2", 32, F32), ("AI", 16, I32),
        ("SEL", 16, U16), ("CODE", 8, U16), ("N1t", 16, U16), ("BS", 256, BF), ("OH", 128, BF), ("MD", 128, BF),
        ("AR", 256, BF), ("PN", 256, BF), ("L0", 256, BF), ("L1", 256, BF)):
    SCRATCH[_n] = ("sbuf", [128, _w], _d)
for _s in range(2):
    for _n, _w, _d in (("S", 4096, BF), ("X", 128, BF), ("XE", 16 * NV, BF), ("OV", 4 * NV, U16), ("OC", 4 * NC, U16),
                       ("DZ", 80, I32), ("DO", 80, I32), ("XO", 32, I32), ("N0t", 16, U16), ("FT", 16, F32), ("TO", 96, F32),
                       ("CM", 4 * NC + 2 * NV, BF), ("ZB", 128, BF),
                       ("OUT", 256, F32), ("ZI", 16, F32), ("ZT", 256, F32)):
        SCRATCH[_n + str(_s)] = ("sbuf", [128, _w], _d)
    for _t in range(4):
        SCRATCH["W%d%d" % (_s, _t)] = ("sbuf", [128, 768], BF)
    for _v in range(2):
        SCRATCH["D%d%d" % (_s, _v)] = ("sbuf", [128, 16 * NV], BF)
        SCRATCH["R%d%d" % (_s, _v)] = ("sbuf", [128, 16 * NV], BF)
SCRATCH["ST"] = ("sbuf", [128, 8, 32], BF)
PSUM = ("K0", "K1", "PO0", "PO1", "AL", "DD", "SM", "N1")
for _n in PSUM:
    SCRATCH[_n] = ("psum", [128, 512], F32)

NDMA = 40
SEMAPHORES = (["sV", "sA", "sP", "sG", "sL", "dF"] + ["d%d" % k for k in range(NDMA)]
              + ["arr%d%d" % (s, t) for s in range(2) for t in range(4)])


def rank_program(g, core, T, topo):
    rank = T.rank_of(core)
    if rank is None:
        return
    NR_ = len(T.cores)
    queues = {"V": g.vector, "A": g.scalar, "P": g.tensor, "G": g, "S": g.sync}

    ops, last, ndma, sent, compn, begun = [], {}, [0], [0], {}, []

    def norm(x):
        if isinstance(x, str):
            return (x, 0, 1 << 30)
        return x

    def op(q, fn, r=(), w=(), comp=None, amt=1):
        me = len(ops)
        deps = set()
        rr, ww = [norm(x) for x in r], [norm(x) for x in w]
        for name, a, b in rr:
            for (a2, b2, o, iw) in last.get(name, []):
                if name in PSUM:
                    if ops[o]["q"] != q:
                        deps.add(o)
                elif iw and a < b2 and a2 < b:
                    deps.add(o)
        for name, a, b in ww:
            for (a2, b2, o, iw) in last.get(name, []):
                if name in PSUM:
                    if ops[o]["q"] != q or q != "P":
                        deps.add(o)
                elif a < b2 and a2 < b:
                    deps.add(o)
        for name, a, b in ww:
            ps = name in PSUM
            last[name] = [e for e in last.get(name, []) if not (ps or (a <= e[0] and e[1] <= b))] + [(a, b, me, True)]
        for name, a, b in rr:
            last.setdefault(name, []).append((a, b, me, False))
        comp = comp or q
        ci = compn.get(comp, 0)
        compn[comp] = ci + 1
        deps.discard(me)
        ops.append({"q": q, "fn": fn, "deps": deps, "comp": comp, "ci": ci, "amt": amt, "sig": amt != 1, "need": []})

    def dma(q, out, in_, r=(), w=(), comp=None):
        if comp is None:
            comp = "d%d" % ndma[0]
            ndma[0] += 1
        qq = queues[q]
        op(q, lambda: qq.dma_start(out, in_), r, w, comp, 16)

    def V(name, r, w, *a, **k):
        fn = {"tt": g.vector.tensor_tensor, "ts": g.vector.tensor_scalar, "cp": g.vector.tensor_copy, "tr": g.vector.transpose,
              "scan": g.vector.tensor_tensor_scan, "set": g.vector.memset}[name]
        op("V", lambda: fn(*a, **k), r, w)

    def A(r, w, out, in_, func, **k):
        op("A", lambda: g.scalar.activation(out, in_, func, **k), r, w)

    def mm(r, bank, out, lhsT, rhs, start=False, stop=False):
        op("P", lambda: g.tensor.matmul(out, lhsT, rhs, start, stop), r, [bank])

    def iota(w, out, pattern, base, cm, small=True):
        if small:
            op("G", lambda: g.iota(out, pattern, base, cm, allow_small_or_imprecise_dtypes=True), (), w)
        else:
            op("G", lambda: g.iota(out, pattern, base, cm), (), w)

    def send(s, t):
        dst = T.cores[(rank - 1 - t % (NR_ - 1)) % NR_]
        rid, pid, _ = topo.addr(dst)
        m = topo.mask(core, dst)
        sent[0] += len(topo.engines(core, dst))
        w = "W%d%d" % (s, t)
        op("G", lambda: g.remote_dma(T[w][:, 256:512], T[w][:, 0:256], T.sem["arr%d%d" % (s, t)], T.sem.sL, pid, rid, m),
           [(w, 0, 256)], (), "sL", 0)

    def recv(s, t):
        src = T.cores[(rank + 1 + t % (NR_ - 1)) % NR_]
        op("N", None, (), [("W%d%d" % (s, t), 256, 512)], "arr%d%d" % (s, t), len(topo.engines(src, core)))

    def half(h):
        return slice(64 * h, 64 * h + 64)

    for s in range(2):
        dma("SA"[s], T.RI[0:64, 256 * s:256 * s + 256], T.resid[half(s), :], (), [("RI", s, s + 1)])
        dma("AS"[s], T.TBi[64:128, 16 * s:16 * s + 16], T.src0[half(s), :], (), [("TBi", s, s + 1)])
    for s in range(2):
        for h in range(2):
            dma("SA"[h], T.NI[half(h), 16 * s:16 * s + 16], T.nx0[half(s), :], (), [("NI", 2 * s + h, 2 * s + h + 1)])
            dma("SA"[h], T["X%d" % s][half(h), :], T.obs[half(s), 128 * h:128 * h + 128], (), [("X%d" % s, h, h + 1)])
    for h in range(2):
        dma("SA"[h], T.S0[half(h), :], T.prof[half(0), :], (), [("S0", h, h + 1)])
    for k in range(16):
        h, al, s, e = k >> 3, (k >> 2) & 1, (k >> 1) & 1, k & 1
        p0, gr = 64 * h + 32 * al + 16 * s, 4 * s + 2 * al + e
        dma("S", T.ZF[p0:p0 + 16, 16 * e:16 * e + 16], T.fit0[gr:gr + 1, :], (), [("ZF", k, k + 1)], "dF")

    def C(k):
        return T.CF[:, k:k + 1]

    def bits(k, sh, m):
        V("ts", ["ip"], [("ic", k, k + 1)], T.ic[:, k:k + 1], T.ip[:], sh, m, OP.arith_shift_right, OP.bitwise_and)

    def col(k, s, m, a):
        V("ts", [("ic", s, s + 1)], [("CF", k, k + 1)], C(k), T.ic[:, s:s + 1], float(m), float(a), OP.mult, OP.add)

    def numbers(s, t):
        w = "W%d%d" % (s, t)
        iota([(w, 512, 768)], T[w][:, 512:768], [[1, 256]], 0, 0)
    iota(["ip"], T.ip[:], [[0, 1]], 0, 1, False)
    iota(["CI"], T.CI[:], [[16, 16]], 0, 0)
    numbers(0, 0)
    iota(["gw"], T.gw[:], [[1, 12], [0, 16]], -4, 0)
    iota(["c64"], T.c64[:], [[0, 2], [1, 64]], 0, 0)
    iota(["g32"], T.g32[:], [[1, 8], [0, 32]], 0, 0)
    for k, (sh, m) in enumerate(((0, 15), (4, 3), (6, 1), (5, 3), (4, 1), (3, 6))):
        bits(k, sh, m)
    col(7, 0, 1, 0)
    col(0, 0, 1, 1)
    V("ts", ["CI", ("CF", 7, 8)], ["CI"], T.CI[:], T.CI[:], C(7), None, OP.add)
    col(3, 1, 1, 0)
    for s in range(2):
        V("cp", ["CI"], [("TBi", 2 + s, 3 + s)], T.TBi[0:64, 16 * s:16 * s + 16], T.CI[0:64, :])
    col(5, 4, -1, 1)
    col(6, 4, 1, 0)
    col(8, 2, 256, 256)
    col(9, 2, 256, 1)
    V("tt", [("ic", 2, 3), ("ic", 5, 6)], [("CF", 2, 3)], C(2), T.ic[:, 5:6], T.ic[:, 2:3], OP.add)
    for s in range(2):
        V("cp", [("W00", 512, 768)], [("RI", 2 + s, 3 + s)], T.RI[64:128, 256 * s:256 * s + 256], T.W00[64:128, 512:768])
    for s in range(2):
        V("cp", [("TBi", s, s + 1), ("TBi", 2 + s, 3 + s)], [("TB", s, s + 1)], T.TB[:, 16 * s:16 * s + 16], T.TBi[:, 16 * s:16 * s + 16])
        w = "W%d0" % s
        V("cp", [("RI", s, s + 1), ("RI", 2 + s, 3 + s), ("TB", s, s + 1)], [(w, 0, 256)], T[w][:, 0:256],
          T.RI[:, 256 * s:256 * s + 256].indirect(T.TB[:, 16 * s:16 * s + 16]))
        send(s, 0)
    V("ts", ["gw", ("CF", 3, 4)], ["Bw"], T.Bw[:], T.gw[:], C(3), None, OP.is_equal)
    V("ts", ["gw", ("CF", 3, 4)], ["NB"], T.NB[:], T.gw[:], C(3), -1.0, OP.is_equal, OP.mult)
    V("ts", ["g32", ("CF", 2, 3)], ["BX"], T.BX[:], T.g32[:], C(2), 32.0, OP.is_equal, OP.mult)
    V("ts", ["gw", ("CF", 2, 3)], ["BH"], T.BH[:], T.gw[:, 64:192], C(2), 32.0, OP.is_equal, OP.mult)
    V("set", (), ["ones"], T.ones[:], 1.0)
    V("set", (), ["KC"], T.KC[0:1, :], 4096.0)
    bits(6, 4, 7)
    bits(7, 0, 32)
    V("ts", [("CF", 7, 8)], [("CF", 1, 2)], C(1), C(7), 0.0, 256.0, OP.is_equal, OP.mult)
    col(14, 6, 1, 0)
    col(23, 2, -1, 1)
    col(22, 2, -31.0 / 32, 1)
    for k, src, r, m in ((4, T.ic[:, 3:4], ("ic", 3, 4), 16.0), (15, T.ic[:, 7:8], ("ic", 7, 8), 1.0), (16, C(2), ("CF", 2, 3), 16.0)):
        V("ts", [r, ("CF", 7, 8)], [("CF", k, k + 1)], C(k), src, m, C(7), OP.mult, OP.add)
    V("cp", ["ip"], [("CF", 17, 18)], C(17), T.ip[:])
    for k, src in ((18, 4), (20, 15)):
        for b in range(2):
            V("ts", [("CF", 5, 7), ("CF", src, src + 1)], [("CF", k + b, k + b + 1)], C(k + b), C(6 - b), 1000.0, C(src), OP.mult, OP.add)
    V("ts", [("CF", 7, 8), ("CF", 1, 2)], [("CF", 10, 11)], C(10), C(7), 1.0, C(1), OP.is_equal, OP.add)
    for k, m, a in ((11, -255.0 / 65536, 1.0), (12, -127.5 / 65536, 0.0), (13, 1.0 / 16, 0.0)):
        V("ts", [("CF", 1, 2)], [("CF", k, k + 1)], C(k), C(1), m, a, OP.mult, OP.add)

    def keep(out, in_, pattern, cmp, base, cm):
        op("G", lambda: g.affine_select(T[out][:], T[in_][:], pattern, cmp, 0.0, base, cm), [in_], [out])
    keep("ST", "BX", [[0, 8], [1, 32]], OP.is_ge, -16, 0)
    keep("TRI", "Bw", [[1, 192]], OP.is_ge, -64, -1)
    keep("HN", "NB", [[-1, 192]], OP.is_gt, 64, 1)
    keep("IB", "NB", [[1, 192]], OP.not_equal, -64, -1)
    iota(["jm1"], T.jm1[:], [[0, 8], [1, 16]], 1, 0)
    iota(["g4"], T.g4[:], [[0, 2], [1, 4], [0, 16]], 0, 0)
    for k in range(16):
        op("G", lambda k=k: g.affine_select(T.LH[:, 128 * k:128 * k + 128], T.BH[:], [[0, 8], [-1, 16]], OP.is_ge, 0.0, k, 0),
           ["BH"], [("LH", k, k + 1)])
    numbers(1, 0)
    for s in range(2):
        for k, c in ((0, 0), (2, 1), (4, 416)):
            iota([("DZ%d" % s, k, k + 1)], T["DZ%d" % s][:, k:80:5], [[0, 16]], c, 0, False)
    for s in range(2):
        for k in range(16):
            A(["X%d" % s], [("XE%d" % s, k, k + 1)], T["XE%d" % s][:, k:16 * NV:16], T["X%d" % s][:, 0:NV], AF.Copy)
    J = T.jm1[:, 0:128]
    for s in range(2):
        V("cp", [("NI", 2 * s, 2 * s + 2)], ["N0t%d" % s], T["N0t%d" % s][:], T.NI[:, 16 * s:16 * s + 16])
        V("cp", [("NI", 2 * s, 2 * s + 2)], [("DO%d" % s, 1, 2)], T["DO%d" % s][:, 1:80:5], T.NI[:, 16 * s:16 * s + 16])
    V("ts", ["gw", "CF"], ["WM"], T.WM[:], T.gw[:, 64:192], C(14), C(10), OP.is_equal, OP.mult)
    num, rnum = T.W00[:, 512:640], ("W00", 512, 768)
    for k in range(6):
        o, a, b = (T.ODD[:, k:4 * NC:4], NV, 128) if k < 4 else (T.ODD[:, 4 * NC + NV * (k - 4):4 * NC + NV * (k - 3)], 0, NV)
        A([rnum, ("CF", 9, 10)], [("ODD", k, k + 1)], o, T.W00[:, 512 + a:512 + b], AF.Identity, bias=C(9), scale=2.0)

    def keyconsts():
        for b in range(2):
            for e in range(2):
                k = 2 * b + e
                V("ts", ["c64", "CF"], [("SN", k, k + 1)], T.SN[:, 128 * k:128 * k + 128], T.c64[:], C(20 + b), 16.0 * e,
                  OP.subtract, OP.is_equal)
        V("ts", [rnum, "CF"], ["P22"], T.P22[:], num, C(16), float(2 ** 22), OP.is_equal, OP.mult)
        V("ts", [rnum, "CF"], [("IH", 0, 1)], T.IH[:, 0:128], num, C(17), C(23), OP.is_equal, OP.mult)
        V("ts", [rnum, "CF"], [("IH", 1, 2)], T.IH[:, 128:256], T.W00[:, 576:704], C(17), None, OP.is_equal)
        V("set", (), ["SM"], T.SM[:, 48:64], 0.0)
        V("ts", ["gw", "CF"], ["BD"], T.BD[:], T.gw[:, 64:192], C(14), C(22), OP.is_equal, OP.mult)
        V("cp", [rnum], ["EX"], T.EX[:], T.W00[:, 512:528])
        for b in range(2):
            V("ts", ["c64", "CF"], [("SW", b, b + 1)], T.SW[:, 128 * b:128 * b + 128], T.c64[:], C(18 + b), None, OP.is_equal)
        for s in range(2):
            do = "DO%d" % s
            V("ts", ["CI", "CF"], [(do, 2, 3)], T[do][:, 2:80:5], T.CI[:], -1.0, C(8), OP.mult, OP.add)
            V("cp", ["CI"], [(do, 3, 4)], T[do][:, 3:80:5], T.CI[:])
        for k in range(15):
            V("cp", ["ST"], [("LG", k, k + 1)], T.LG[:, 128 * k:128 * k + 128], T.ST[:, :, 15 - k:31 - k])

    def lastconsts():
        V("ts", ["jm1"], ["RS"], T.RS[:], J, 1.0, BIG, OP.is_equal, OP.mult)
        V("ts", ["g4", "CF"], ["B2x"], T.B2x[:], T.g4[:], C(3), 32.0, OP.is_equal, OP.mult)
        for k in range(2):
            V("ts", ["jm1", "CF"], [("MK", k, k + 1)], T.MK[:, 128 * k:128 * k + 128], J, C(0), None, OP.is_equal)
        V("ts", ["RS"], ["RS"], T.RS[:], T.RS[:], -1.0, None, OP.add)

    def fit(step):
        if step == 0:
            V("ts", ["ZF"], ["ZG"], T.ZG[:], T.ZF[:], 32.0, None, OP.mult)
        if step == 1:
            V("tr", ["ZG"], ["ZH"], T.ZH[:], T.ZG[:])
        for s in range(2 if step == 2 else 0):
            V("cp", ["ZH"], [("XO%d" % s, 1, 2)], T["XO%d" % s][:, 16:32], T.ZH[:, 16 * s:16 * s + 16])
            V("cp", ["ZH"], ["FT%d" % s], T["FT%d" % s][:], T.ZH[:, 16 * s:16 * s + 16])

    def wide(name, h):
        return T[name][0:64, 64 - 64 * h:192 - 64 * h]

    def places(c, v):
        o = T.PO1[:, 4 * NC + NV * v:4 * NC + NV * v + NV] if c else T.PO0[:, NV * v:NV * v + NV]
        return (("PO%d" % c, o, 0, NV), ("PO1", T.PO1[:, 2 * c + v:4 * NC:4], NV, 128))

    def pos0(s):
        cm, zb = "CM%d" % s, "ZB%d" % s
        mm(["WM", cm], "PO0", T.PO0[:, 0:2 * NV], T.WM[:], T[cm][:, 4 * NC:4 * NC + 2 * NV], True)
        mm(["WM", cm], "PO1", T.PO1[:, 0:4 * NC + 2 * NV], T.WM[:], T[cm][:], True)
        for c in range(2):
            mm(["WM", zb], "AL", T.AL[:, c:256:2], T.WM[:], T[zb][:], c == 0)

    def mass(s):
        w, cm, zb, bank = "W%d0" % s, "CM%d" % s, "ZB%d" % s, ("DD", "SM")[s]
        ib, ri = T.IO[:, 128 * s:128 * s + 128], ("IO", 128 * s, 128 * s + 128)
        mm(["KC", "ones"], bank, T[bank][:, 0:128], T.KC[0:1, :], T.ones[0:1, 0:128], True)
        for h in range(2):
            mm(["Bw", (w, 0, 256)], bank, T[bank][:, 0:128], wide("Bw", h), T[w][0:64, 128 * h:128 * h + 128], False, h == 1)
        A(["ones", "CF"], [cm], T[cm][:], T.ones[:, 0:4 * NC + 2 * NV], AF.Copy, scale=C(13))

        def spread():
            V("cp", [ri], [zb], T[zb][:], ib)
            A([zb], [cm], T[cm][:, 4 * NC + NV:], T[zb][:, 0:NV], AF.Copy)
            for c in range(2):
                A([zb], [cm], T[cm][:, 2 * c + 1:4 * NC:4], T[zb][:, NV:128], AF.Copy)
        return [lambda: V("ts", [bank, "CF"], [ri], ib, T[bank][:, 0:128], C(11), C(12), OP.mult, OP.add),
                lambda: V("ts", [ri], [ri], ib, ib, 255, None, OP.bitwise_and), spread]

    def pos1(c, part, stop):
        L = "L%d" % c
        for v in range(2):
            bank, o, a, b = places(c, v)[part]
            m = "HN" if v else "TRI"
            for h in range(2):
                mm([m, L], bank, o, wide(m, h), T[L][0:64, 128 * h + a:128 * h + b], False, stop and v == 1 and h == 1)

    def allowed_mm():
        for c in range(2):
            for h in range(2):
                mm(["IB", "L%d" % c], "AL", T.AL[:, c:256:2], wide("IB", h), T["L%d" % c][0:64, 128 * h:128 * h + 128],
                   False, c == 1 and h == 1)

    def lists(s, t, c):
        w, n = "W%d%d" % (s, t), ("N1t" if c else "N0t%d" % s)
        A([(w, 256, 512), n], ["L%d" % c], T["L%d" % c][:], T[w][:, 256:512].indirect(T[n][:, 0:16]), AF.Copy)

    def offsets(bank, p0, q0, o, o0, n, i0):
        ib, ri = T.IO[:, i0:i0 + n], ("IO", i0, i0 + n)
        return [lambda: V("tt", [bank, "ODD"], [ri], ib, T[bank][:, p0:p0 + n], T.ODD[:, q0:q0 + n], OP.mult),
                lambda: V("ts", [ri], [ri], ib, ib, 2, 4095, OP.arith_shift_right, OP.bitwise_and),
                lambda: move(T[o][:, o0:o0 + n], ib, n, [ri], [(o, o0, o0 + n)])]

    def move(out, in_, n, r, w, urgent=False):
        if begun and not urgent:
            op("G", lambda: g.affine_select(out, in_, [[0, n]], OP.is_ge, 0.0, 0, 0), r, w)
        else:
            V("cp", r, w, out, in_)

    def mix(*chains):
        for k in range(max(len(c) for c in chains)):
            for c in chains:
                if k < len(c):
                    c[k]()

    def head1(s, t):
        recv(s, t)
        lists(s, t, 0)
        pos1(0, 0, True)
        pos1(0, 1, False)

    def second():
        V("tr", ["L0"], ["NT"], T.NT[64:128, :], T.L0[64:128, :])
        for b in range(2):
            for e in range(2):
                k = 128 * (2 * b + e)
                mm(["SN", "NT"], "N1", T.N1[:, b:16:2], T.SN[64:128, k:k + 128], T.NT[64:128, 16 * e:256:32], e == 0, e == 1)

    def head2(s):
        do = "DO%d" % s
        o = offsets("PO0", 0, 4 * NC, "OV%d" % s, 0, 2 * NV, 0)
        o[0]()
        V("cp", ["N1"], ["N1t"], T.N1t[:], T.N1[:, 0:16])
        V("tt", ["N1", (do, 1, 2)], [(do, 0, 1)], T[do][:, 0:80:5], T.N1[:, 0:16], T[do][:, 1:80:5], OP.subtract)
        o[1]()
        V("cp", ["N1"], [("XO%d" % s, 0, 1)], T["XO%d" % s][:, 0:16], T.N1[:, 0:16])
        o[2]()

    def head3(s, t):
        lists(s, t, 1)
        pos1(1, 1, False)
        pos1(1, 0, True)

    def head4(s):
        mix(*[offsets("PO1", k, k, "OC%d" % s, k, 2 * NC, 2 * NV + k) for k in (0, 2 * NC)])

    def head5(s):
        return offsets("PO1", 4 * NC, 4 * NC, "OV%d" % s, 2 * NV, 2 * NV, 2 * NV + 4 * NC)

    def gat(s, c, v, a=0, b=NV):
        d, o, k = "D%d%d" % (c, v), "OV%d" % s, NV * (2 * c + v)
        if a == b:
            return
        V("tt", ["S%d" % s, "XE%d" % s, (o, k + a, k + b)], [(d, a, b)], T[d][:, 16 * a:16 * b],
          T["S%d" % s][:, 0:4096].indirect(T[o][:, k + a:k + b]), T["XE%d" % s][:, 16 * a:16 * b], OP.subtract)

    def neg(c, v, a=0, b=NV):
        d, r = "D%d%d" % (c, v), "R%d%d" % (c, v)
        V("ts", [(d, a, b)], [(r, a, b)], T[r][:, 16 * a:16 * b], T[d][:, 16 * a:16 * b], 0.0, -2.0, OP.min, OP.mult)

    def size(a, b):
        A([("D11", a, b)], [("D11", a, b)], T.D11[:, 16 * a:16 * b], T.D11[:, 16 * a:16 * b], AF.Abs)

    def keys(s, b, c, v, stop=False):
        d, l, K = "%s%d%d" % (b, c, v), ("LH" if v else "LG"), "K%d" % s
        for k in range(15 + v):
            mm([(l, k, k + 1), d], K, T[K][:, c:2 * NV:2], T[l][:, 128 * k:128 * k + 128], T[d][:, k:16 * NV:16],
               d == "D00" and k == 0, stop and k == 14 + v)

    def cslots(s, a, b):
        for i in range(a, b):
            A(["S%d" % s, "OC%d" % s, "X%d" % s], [("CD", i, i + 1)], T.CD[:, 64 * i:64 * i + 64],
              T["S%d" % s][:, 0:4096].indirect(T["OC%d" % s][:, 4 * i:4 * i + 4]), AF.Abs, bias=T["X%d" % s][:, NV + i:NV + i + 1], scale=-1.0)

    def keysc(s, a, b, stop=False):
        K = "K%d" % s
        for v in range(2 if a < b else 0):
            l = "LH" if v else "LG"
            for k in range(15 + v):
                mm([(l, k, k + 1), ("CD", a, b)], K, T[K][:, 2 * (NV + a):2 * (NV + b)], T[l][:, 128 * k:128 * k + 128],
                   T.CD[:, 64 * a + 16 * v + k:64 * b:32], False, stop and v == 1 and k == 15)

    def penalty(s):
        V("ts", ["AR"], ["PN"], T.PN[:], T.AR[:], 127.5, None, OP.is_gt)
        for x in (slice(0, 2 * NV, 2), slice(1, 2 * NV, 2), slice(2 * NV, 256)):
            mm(["P22", "PN"], "K%d" % s, T["K%d" % s][:, x], T.P22[:], T.PN[:, x])

    def best(s):
        K = "K%d" % s
        return [lambda: (A([K], ["K0S"], T.K0S[:], T[K][:, 0:256:2], AF.Identity, bias=-16.0),
                         V("tt", [K, "K0S"], ["km"], T.km[:], T[K][:, 1:256:2], T.K0S[:], OP.min)),
                lambda: V("tr", ["km"], ["XT"], T.XT[:], T.km[:]),
                lambda: V("scan", ["RS", "XT"], ["Y"], T.Y[:], T.RS[:], T.XT[:], BIG, OP.add, OP.min)]

    def finish(s, t, slots):
        sel = select(s, t)
        return (best(s) + [swap, sel[0], lambda: (sel[1](), slots(), site())] + sel[2:4]
                + [lambda: (sel[4](), gap(), tally(t)), delta, lambda: newlists(s, t)])

    def swap():
        for h in range(2):
            V("ts", ["Y"], [("YH", h, h + 1)], T.YH[:, 4 * h:4 * h + 4], T.Y[:, 15 + 16 * h:128:32], 31.0, None, OP.add)
        for b in range(2):
            mm(["SW", "YH"], "SM", T.SM[:, b:16:2], T.SW[:, 128 * b:128 * b + 128], T.YH[:], True, True)

    def select(s, t):
        dz, do, w = "DZ%d" % s, "DO%d" % s, "W%d%d" % (s, t)
        key = T[do][:, 4:80:5]
        return [
            lambda: (V("cp", ["SM"], [(do, 4, 5)], key, T.SM[:, 0:16]),
                     V("tt", ["SM", "FT%d" % s], [(dz, 3, 4)], T[dz][:, 3:80:5], T.SM[:, 0:16], T["FT%d" % s][:], OP.is_lt)),
            lambda: (V("ts", [(do, 4, 5)], [(dz, 1, 2)], T[dz][:, 1:80:5], key, 4, 1, OP.arith_shift_right, OP.bitwise_and),
                     [V("ts", [(do, 4, 5)], [("KS", h, h + 1)], T.KS[half(h), :], T[do][half(h), 4 + 40 * h:40 + 40 * h:5], 15, None,
                        OP.bitwise_and) for h in range(2)],
                     V("ts", [(do, 4, 5)], [("U", 1, 2)], T.U[:, 16:32], key, 0x7FFFFFE0, None, OP.bitwise_and),
                     move(T.CODE[:], T.KS[:], 8, ["KS"], ["CODE"]),
                     [move(T.AC[:, 16 * k:16 * k + 16], T[dz][:, 3:80:5], 16, [(dz, 3, 4)], [("AC", k, k + 1)]) for k in range(2)]),
            lambda: V("scan", [(dz, 0, 5), (do, 0, 5)], ["FS"], T.FS[:], T[dz][:, 0:80], T[do][:, 0:80], 0.0, OP.mult, OP.add),
            lambda: (V("cp", ["FS"], ["SEL"], T.SEL[:], T.FS[:, 3:80:5]),
                     V("ts", ["FS"], [("U", 0, 1)], T.U[:, 0:16], T.FS[:, 4:80:5], 5, 255, OP.arith_shift_right, OP.bitwise_and)),
            lambda: (V("cp", [w, "SEL"], ["BS"], T.BS[:], T[w][:, 0:768].indirect(T.SEL[:, 0:16])) if (s, t) == (1, 3) else
                     A([w, "SEL"], ["BS"], T.BS[:], T[w][:, 0:768].indirect(T.SEL[:, 0:16]), AF.Copy))]

    def site():
        A(["MK", "CODE"], ["OH"], T.OH[:], T.MK[:, 0:16].indirect(T.CODE[:, 0:8]), AF.Copy)

    def distance():
        A(["AL"], ["AR"], T.AR[:], T.AL[:, 0:256], AF.Abs, bias=-4223.5)

    def own(s):
        w = "W%d0" % s
        for h in range(2):
            mm(["Bw", (w, 0, 256)], "DD", T.DD[:, 0:128], wide("Bw", h), T[w][0:64, 128 * h:128 * h + 128], h == 0)

    def gap():
        for h in range(2):
            mm(["NB", "BS"], "DD", T.DD[:, 0:128], wide("NB", h), T.BS[0:64, 128 * h:128 * h + 128], False, h == 1)

    def delta():
        V("tt", ["DD", "OH"], ["MD"], T.MD[:], T.DD[:, 0:128], T.OH[:], OP.mult)
        for h in range(2):
            mm(["IH", "MD"], "N1", T.N1[:, 256 + 128 * h:384 + 128 * h], T.IH[:, 128 * h:128 * h + 128], T.MD[:], True, True)

    def newlists(s, t):
        if t < 3:
            w = "W%d%d" % (s, t + 1)
            V("tt", ["N1", "BS"], [(w, 0, 256)], T[w][:, 0:256], T.N1[:, 256:512], T.BS[:], OP.add)
            send(s, t + 1)
        else:
            o = "OUT%d" % s
            V("tt", ["N1", "BS"], [o], T[o][0:64, :], T.N1[0:64, 256:512], T.BS[0:64, :], OP.add)
            dma("S", T.yr[half(s), :], T[o][0:64, :], [o], ())

    def tally(t):
        if t < 3:
            mm(["B2x", ("AC", 0, 1)], "SM", T.SM[:, 32:48], T.B2x[0:64, :], T.AC[0:64, 0:16], True, True)

    def post1(s, t):
        xo, to = "XO%d" % s, "TO%d" % s

        def first():
            V("tt", ["U", xo], ["E1"], T.E1[:], T.U[:], T[xo][:], OP.subtract)
            if t < 3:
                V("scan", ["SM", "ones", to], [(to, t, t + 1)], T[to][:, 32 * t:32 * t + 32], T.ones[:, 0:32], T.SM[:, 32:64],
                  T[to][:, 32 * t - 1:32 * t] if t else 0.0, OP.mult, OP.add)

        def middle():
            V("tt", ["E1", "AC"], ["E2"], T.E2[:], T.E1[:], T.AC[:], OP.mult)
            if t < 3:
                move(T.AI[:], T[to][:, 32 * t + 16:32 * t + 32], 16, [to], ["AI"])

        def last():
            if t < 3:
                V("tt", ["E2", xo], [xo], T[xo][:], T.E2[:], T[xo][:], OP.add)
            for h in range(2 if t == 3 else 0):
                V("tt", ["E2", xo], [("ZI%d" % s, h, h + 1)], T["ZI%d" % s][half(h), :], T.E2[half(h), 16 * h:16 * h + 16],
                  T[xo][half(h), 16 * h:16 * h + 16], OP.add)
        return [first, middle, last]

    def post2(s, t):
        do, xo = "DO%d" % s, "XO%d" % s
        if t < 3:
            move(T["N0t%d" % s][:], T[xo][:, 0:16], 16, [xo], ["N0t%d" % s])
            move(T[do][:, 1:80:5], T[xo][:, 0:16], 16, [xo], [(do, 1, 2)])
            numbers(s, t + 1)

    def post3(s, t):
        xo = "XO%d" % s
        if t < 3:
            return [lambda: V("ts", ["AI"], ["AM"], T.AM[:], T.AI[:], 255, None, OP.bitwise_and),
                    lambda: V("tt", [xo, "AM"], ["FT%d" % s], T["FT%d" % s][:], T[xo][:, 16:32], T.AM[:], OP.subtract)]
        zi, zt, bank = "ZI%d" % s, "ZT%d" % s, "PO%d" % s

        def rows():
            V("tt", [zi, "EX", "MK"], ["ZX"], T.ZX[:], T[zi][:, 0:16].indirect(T.EX[:, 0:16]), T.MK[:], OP.mult)

        def store():
            mm(["BD", "ZX"], bank, T[bank][:, 0:256], T.BD[:], T.ZX[:], True, True)
            A([bank], [zt], T[zt][:], T[bank][:, 0:256], AF.Copy)
            dma("SA"[s], T.yn[4 * s:4 * s + 4, :], T[zt][0:64:16, :], [zt], ())
            dma("SA"[s], T.yf[4 * s:4 * s + 4, :], T[zt][64:128:16, :], [zt], ())
        return [lambda: None, rows, store]

    mix(mass(0), mass(1))
    pos0(0)
    keyconsts()
    head1(0, 0)
    for h in range(2):
        dma("S", T.S1[half(h), :], T.prof[half(1), :], [("W00", 256, 512)], [("S1", h, h + 1)])
    second()
    head2(0)
    head3(0, 0)
    gat(0, 0, 0, 0, G0)
    head4(0)
    for p in range(8):
        s, y = p % 2, 1 - p % 2
        tail, ty = p >= 1, (p - 1) // 2
        head, th = p < 7, (p + 1) // 2
        allowed_mm()
        gat(s, 0, 0, 0 if tail else G0, NV)
        cslots(s, 0, A1)
        keys(s, "D", 0, 0)
        later = post1(y, ty) + post3(y, ty) if tail else [lambda: None] * 2 + [lambda k=k: fit(k) for k in range(3)]
        h5, cut = head5(s), [NV * k // 5 for k in range(6)]
        piece = [lambda k=k: neg(0, 0, cut[k], cut[k + 1]) for k in range(5)]
        part = [lambda a=a, b=b: gat(s, 0, 1, a, b) for a, b in ((0, GA), (GA, GB), (GB, NV))]
        mix([lambda: (h5[0](), piece[0]()), lambda: (h5[1](), h5[2](), distance()), piece[1], piece[2],
             lambda: (part[0](), pos0(y) if head else None, own(y) if tail else None), piece[3], lambda: (piece[4](), keys(s, "R", 0, 0)), lambda: penalty(s),
             lambda: None, part[1], lambda: (later[0](), part[2]())],
            finish(y, ty, lambda: cslots(s, A1, A2)) if tail else [lambda: cslots(s, A1, A2), lastconsts])
        begun.append(p)
        cslots(s, A2, CB)
        keysc(s, 0, CB)
        keys(s, "D", 0, 1)
        later[1]()
        neg(0, 1)
        later[2]()
        keys(s, "R", 0, 1)
        if tail:
            post2(y, ty)
        gat(s, 1, 0)
        keys(s, "D", 1, 0)
        later[3]()
        cslots(s, CB, A4)
        if head:
            head1(y, th)
        gat(s, 1, 1, 0, G1)
        if head:
            later[4]()
        neg(1, 0)
        gat(s, 1, 1, G1, G2)
        if head:
            second()
        keys(s, "R", 1, 0)
        gat(s, 1, 1, G2, G3 if head else G2)
        if head:
            head2(y)
        cslots(s, A4, A5)
        if head:
            head3(y, th)
        if head:
            cslots(s, A5, NC)
            keysc(s, CB, NC)
            size(0, G3)
            gat(s, 1, 1, G3, NV)
            head4(y)
            size(G3, NV)
        else:
            cslots(s, A5, NC)
            keysc(s, CB, NC)
            size(0, G2)
            for a, b in ((G2, NV - GL), (NV - GL, NV)):
                gat(s, 1, 1, a, b)
                size(a, b)
        keys(s, "D", 1, 1, True)
    steps = finish(1, 3, lambda: None)
    one, two = post1(1, 3), post3(1, 3)
    mix(later[4:5] + steps[:2] + later[5:] + [lambda: own(1)] + steps[2:8] + [one[0], steps[8], one[1], one[2], steps[9], two[1], steps[10], two[2]])

    known = {}
    for o in ops:
        kn = known.setdefault(o["q"], {}) if o["q"] != "N" else {}
        for d in sorted(o["deps"], reverse=True):
            p = ops[d]
            if kn.get(p["comp"], -1) >= p["ci"]:
                continue
            o["need"].append(d)
            p["sig"] = True
            for c, v in p["clock"].items():
                if kn.get(c, -1) < v:
                    kn[c] = v
            kn[p["comp"]] = max(kn.get(p["comp"], -1), p["ci"])
        o["clock"] = dict(kn)
    names = {"V": "sV", "A": "sA", "P": "sP", "G": "sG"}
    count = {}
    for o in ops:
        c = names.get(o["comp"], o["comp"])
        q = queues.get(o["q"])
        for d in o["need"]:
            p = ops[d]
            q.wait_ge(T.sem[names.get(p["comp"], p["comp"])], p["val"])
        if o["q"] == "N":
            count[c] = count.get(c, 0) + o["amt"]
            o["val"] = count[c]
            continue
        ins = o["fn"]()
        if o["comp"] == "sL":
            continue
        if o["sig"]:
            count[c] = count.get(c, 0) + o["amt"]
            o["val"] = count[c]
            ins.then_inc(T.sem[c], o["amt"])
    for c in count:
        g.wait_ge(T.sem[c], count[c])
    g.wait_ge(T.sem.sL, sent[0])
